import numpy as np
import ml_dtypes


def mxq(x, axis, fmt="e4m3"):
    dtype, down = {"e4m3": (ml_dtypes.float8_e4m3fn, 7), "e5m2": (ml_dtypes.float8_e5m2, 14)}[fmt]
    v = np.moveaxis(np.asarray(x, np.float32).astype(ml_dtypes.bfloat16).astype(np.float64), axis, -1)
    blocks = v.reshape(v.shape[:-1] + (-1, 32))
    amax = np.abs(blocks).max(-1, keepdims=True)
    byte = np.maximum(np.where(amax > 0, np.frexp(amax)[1] - 1 + 127, 0) - down, 1)
    scale = np.exp2(byte - 127.0)
    codes = (blocks / scale).astype(np.float32).astype(dtype).astype(np.float64)
    return np.moveaxis((codes * scale).reshape(v.shape), -1, axis)


WIDE = False


def mx_kscale(k):
    if not WIDE:
        return np.ones(k)
    levels = np.array([10, -10, 5, -5, 0])
    if k % 512:
        return np.exp2(np.random.permutation(np.resize(levels, k // 32))).repeat(32)
    a = np.empty((k // 512, 16))
    for p in range(k // 512):
        a[p, :8] = np.random.permutation(np.resize(levels, 8))
        for g in range(8):
            far = levels[np.abs(levels - a[p, g]) >= 10]
            a[p, g + 8] = far[np.random.randint(len(far))]
    return np.exp2(a.ravel()).repeat(32)


BF16 = ml_dtypes.bfloat16


def bf(x):
    return np.asarray(x, np.float32).astype(BF16)


def f64(x):
    return np.asarray(x).astype(np.float64)


E2M1 = np.array([0.0, 0.5, 1.0, 1.5, 2.0, 3.0, 4.0, 6.0, -0.0, -0.5, -1.0, -1.5, -2.0, -3.0, -4.0, -6.0])


def pack_weight(w, fmt):
    k, n = w.shape
    w = f64(bf(w)).reshape(k // 32, 32, n)
    amax = np.abs(w).max(1)
    if fmt == "e4m3":
        byte = np.frexp(amax)[1] - 1 + 127 - 7
    else:
        mant, ex = np.frexp(amax / 6.0)
        byte = np.where(mant > 0.5, ex, ex - 1) + 127
    byte = np.clip(np.where(amax > 0, byte, 1), 1, 254)
    scaled = (w * np.exp2(127.0 - byte)[:, None, :]).reshape(k, n).astype(np.float32)
    by_word = np.ascontiguousarray(scaled.reshape(k // 512, 128, 4, n).transpose(0, 1, 3, 2))
    if fmt == "e4m3":
        words = by_word.astype(ml_dtypes.float8_e4m3fn).view(np.uint8)
    else:
        c = by_word.astype(ml_dtypes.float4_e2m1fn).view(np.uint8) & 0xF
        words = c[..., 0::2] | (c[..., 1::2] << 4)
    return np.ascontiguousarray(words), np.ascontiguousarray(byte.astype(np.uint8).reshape(k // 512, 16, n))


def unpack_weight(words, scales, fmt):
    g, p, n, _ = words.shape
    if fmt == "e4m3":
        vals = np.ascontiguousarray(words).view(ml_dtypes.float8_e4m3fn).astype(np.float64)
    else:
        nib = np.empty((g, p, n, 4), np.uint8)
        nib[..., 0::2] = words & 0xF
        nib[..., 1::2] = words >> 4
        vals = E2M1[nib]
    vals = vals * np.repeat(np.exp2(scales.astype(np.float64) - 127.0), 8, axis=1)[..., None]
    return vals.transpose(0, 1, 3, 2).reshape(g * 512, n)
def pack4(w):
    words, scales = pack_weight(w, "e2m1")
    return words.reshape(words.shape[0], 128, -1), scales


def unpack4(words, scales):
    return unpack_weight(words.reshape(words.shape[0], 128, -1, 2), scales, "e2m1")


def planes(Y):
    n, m = Y.shape
    b = f64(bf(Y)).reshape(n // 32, 32, m)
    amax = np.abs(b).max(1)
    byte = np.clip(np.where(amax > 0, np.frexp(amax)[1] - 1 + 127 - 7, 1), 1, 254)
    codes = (b * np.exp2(127.0 - byte)[:, None, :]).reshape(n, m).astype(np.float32).astype(ml_dtypes.float8_e4m3fn).view(np.uint8)
    words = codes.reshape(n // 512, 128, 4, m).transpose(0, 1, 3, 2)
    return np.ascontiguousarray(words), np.ascontiguousarray(byte.astype(np.uint8).reshape(n // 512, 16, m))


X, N, Q = 2048, 512, 1024


def entropy_ansatz(alpha, m):
    eta = mxq(alpha, 1, "e4m3") @ m
    return np.exp(eta)


def upwind_face_flux(f, w):
    fp = np.roll(f, -1, axis=0)
    w_pos = np.maximum(w, 0.0)[None, :]
    w_neg = np.minimum(w, 0.0)[None, :]
    return w_pos * f + w_neg * fp


def setup_inputs():
    s, t = mx_kscale(N), mx_kscale(Q)
    alpha = bf(np.random.standard_normal((X, N)) * 0.5 / np.sqrt(N) * s[None, :])
    m_words, m_scales = pack4(np.random.standard_normal((N, Q)) / s[:, None])
    w = bf(np.random.standard_normal(Q) * t)
    p_words, p_scales = pack4(np.random.standard_normal((Q, N)) * 2.0 / np.sqrt(Q) / t[:, None])
    return {
        "alpha": alpha,
        "m_words": m_words,
        "m_scales": m_scales,
        "w": w,
        "p_words": p_words,
        "p_scales": p_scales,
        "u": bf(np.random.standard_normal((X, N))),
        "sigma": bf(np.random.uniform(0.1, 1.0, X)),
    }


def core(alpha, m_words, m_scales, w, p_words, p_scales, u, sigma):
    f = entropy_ansatz(f64(alpha), unpack4(m_words, m_scales))
    flux = upwind_face_flux(f, f64(w))
    d = flux - np.roll(flux, 1, axis=0)
    div = mxq(d, 1, "e4m3") @ unpack4(p_words, p_scales)
    return (f64(u) - 0.5 * div) / (1.0 + f64(sigma))[:, None]


def reference(alpha, m_words, m_scales, w, p_words, p_scales, u, sigma):
    R_out = core(alpha, m_words, m_scales, w, p_words, p_scales, u, sigma)
    words, scales = planes(R_out)
    return R_out, words, scales

@@ -1,0 +1,459 @@
+from contextlib import ExitStack
+
+import concourse.mybir as mybir
+from concourse.masks import make_identity
+
+X, N, Q = 2048, 512, 1024
+FLOPS = 2 * (2 * X * N * Q)
+
+F32 = mybir.dt.float32
+BF16 = mybir.dt.bfloat16
+I32 = mybir.dt.int32
+U32 = mybir.dt.uint32
+U8 = mybir.dt.uint8
+FP8X4 = mybir.dt.float8_e4m3fn_x4
+FP4X4 = mybir.dt.float4_e2m1fn_x4
+
+ALU = mybir.AluOpType
+ACT = mybir.ActivationFunctionType
+
+P = 128
+PACK = 4
+CELLS = P * PACK
+CHUNKS = X // CELLS
+PASSES = Q // (P * PACK)
+PITCH = 136
+ASSIST = {0: (0,), 1: (0,)}
+LEAD = 8
+
+
+def tile_entropyclosuremomentkineticupwindstep_x2_kernel(
+    tc, alpha, m_words, m_scales, w, p_words, p_scales, u, sigma, out_0, out_1, out_2
+):
+    nc = tc.nc
+    with ExitStack() as ctx:
+        keep = ctx.enter_context(tc.tile_pool(name="keep", bufs=1))
+        load = ctx.enter_context(tc.tile_pool(name="load", bufs=CHUNKS))
+        work = ctx.enter_context(tc.tile_pool(name="work", bufs=2))
+        work3 = ctx.enter_context(tc.tile_pool(name="work3", bufs=3))
+        work4 = ctx.enter_context(tc.tile_pool(name="work4", bufs=4))
+        psum_eta = ctx.enter_context(tc.psum_pool(name="psum_eta", bufs=2))
+        psum_misc = ctx.enter_context(tc.psum_pool(name="psum_misc", bufs=3))
+        psum_div = ctx.enter_context(tc.psum_pool(name="psum_div", bufs=3))
+        single = ctx.enter_context(tc.tile_pool(name="single", bufs=1))
+        ctx.enter_context(tc.manual_schedule())
+
+        ident = keep.tile([P, P], F32, name="ident")
+        m_raw = keep.tile([P, 2 * Q], U8, name="m_raw", align_bytes=64)
+        m_plane = keep.tile([P, Q], U8, name="m_plane", align_bytes=64)
+        mw = keep.tile([P, PASSES, PACK, 2 * P], U8, name="mw", align_bytes=64)
+        ms = keep.tile([P, PASSES, PACK, P], U8, name="ms", align_bytes=64)
+        pw = keep.tile([P, PASSES, 2 * N], U8, name="pw", align_bytes=64)
+        ps = keep.tile([P, PASSES, N], U8, name="ps", align_bytes=64)
+        w_sb = keep.tile([P, PASSES, 16], BF16, name="w_sb")
+        s_sb = keep.tile([P, CHUNKS, 16], BF16, name="s_sb")
+        wpos = keep.tile([P, PASSES * PACK], F32, name="wpos")
+        wneg = keep.tile([P, PASSES * PACK], F32, name="wneg")
+        s1 = keep.tile([P, CHUNKS * PACK], F32, name="s1")
+        rden = keep.tile([P, CHUNKS * PACK], F32, name="rden")
+        rneg = keep.tile([P, CHUNKS * PACK], F32, name="rneg")
+        codes = keep.tile([P, CHUNKS, CELLS], U32, name="codes", align_bytes=64)
+        scales = keep.tile([P, CHUNKS, CELLS], U8, name="scales", align_bytes=64)
+        lcodes = keep.tile([P, P], U32, name="lcodes", align_bytes=64)
+        lscales = keep.tile([P, P], U8, name="lscales", align_bytes=64)
+        f_last = keep.tile([P, PASSES, PACK], F32, name="f_last")
+        l_pos = keep.tile([P, PASSES, PACK], F32, name="l_pos")
+        l_neg = keep.tile([P, PASSES, PACK], F32, name="l_neg")
+
+        alpha_rows = alpha.rearrange("(c m t) k -> c m t k", m=P, t=PACK)
+        u_rows = u.rearrange("(c m t) n -> c m t n", m=P, t=PACK)
+        out_rows = out_0.rearrange("(c m t) n -> c m t n", m=P, t=PACK)
+
+        al = [load.tile([P, PACK, N], BF16, name="al") for _ in range(CHUNKS)]
+        al_left = keep.tile([P, N], BF16, name="al_left")
+        ut = [load.tile([P, PACK, N], BF16, name="ut") for _ in range(CHUNKS)]
+
+        nc.vector.memset(m_plane[:].bitcast(I32), 0)
+        nc.vector.memset(ps[:].rearrange("p g n -> p (g n)").bitcast(I32), 0)
+        make_identity(nc, ident[:])
+
+        nc.sync.dma_start(out=al[0][:, 0:2, :], in_=alpha_rows[0, :, 0:2, :])
+        nc.scalar.dma_start(out=w_sb[:, :, 0:PACK], in_=w.rearrange("(h p a) -> p h a", p=P, a=PACK))
+        nc.sync.dma_start(out=al[0][:, 2:4, :], in_=alpha_rows[0, :, 2:4, :])
+        nc.sync.dma_start(out=m_raw[:].bitcast(I32), in_=m_words[0].bitcast(I32))
+        for quad in range(4):
+            nc.scalar.dma_start(
+                out=m_plane[32 * quad : 32 * quad + 4, :].bitcast(I32),
+                in_=m_scales[0, 4 * quad : 4 * quad + 4, :].bitcast(I32),
+            )
+        nc.sync.dma_start(out=al_left[:], in_=alpha[X - P : X, :])
+        nc.sync.dma_start(out=al[1][:], in_=alpha_rows[1])
+        nc.scalar.dma_start(out=s_sb[:, :, 0:PACK], in_=sigma.rearrange("(c m t) -> m c t", m=P, t=PACK))
+        nc.sync.dma_start(out=ut[0][:], in_=u_rows[0])
+        nc.sync.dma_start(out=pw[:].bitcast(I32), in_=p_words.bitcast(I32).rearrange("g p b -> p g b"))
+        for quad in range(4):
+            nc.sync.dma_start(
+                out=ps[32 * quad : 32 * quad + 4, :, :].bitcast(I32),
+                in_=p_scales.bitcast(I32)[:, 4 * quad : 4 * quad + 4, :].rearrange("g r n -> r g n"),
+            )
+        for c in range(2, CHUNKS):
+            nc.sync.dma_start(out=al[c][:], in_=alpha_rows[c])
+            nc.sync.dma_start(out=ut[c - 1][:], in_=u_rows[c - 1])
+        nc.sync.dma_start(out=ut[CHUNKS - 1][:], in_=u_rows[CHUNKS - 1])
+
+        def permute_m(h):
+            raw = m_raw[:, h * N * 2 : (h + 1) * N * 2].rearrange("p (m a b) -> p a m b", a=PACK, b=2)
+            nc.vector.tensor_copy(out=mw[:, h].rearrange("p a (m b) -> p a m b", b=2), in_=raw)
+            plane = m_plane[:, h * N : (h + 1) * N].rearrange("p (m a) -> p a m", a=PACK)
+            nc.vector.tensor_copy(out=ms[:, h], in_=plane)
+
+        def turn_half(c, half, engine):
+            words = al[c][:].bitcast(F32)
+            bank = psum_misc.tile([P, 2, 2, P], F32, name="bank", tag="misc")
+            for t in range(2):
+                for e in range(2):
+                    nc.tensor.transpose(bank[:, t, e, :], words[:, 2 * half + t, e : N // 2 : 2], ident[:])
+            grouped = work4.tile([P, 2 * P, PACK], BF16, name="grouped", align_bytes=64)
+            dst = grouped[:].bitcast(F32).rearrange("p (t m) e -> p t m e", t=2)
+            src = bank[:].rearrange("p t e m -> p t m e")
+            if engine == "v":
+                nc.vector.tensor_copy(out=dst, in_=src)
+            else:
+                nc.scalar.copy(out=dst, in_=src)
+            return grouped
+
+        def quant_half(c, half, grouped):
+            cols = slice(half * 2 * P, (half + 1) * 2 * P)
+            nc.vector.quantize_mx(
+                out=codes[:, c, cols].bitcast(FP8X4),
+                scales=scales[:, c, cols],
+                in_=grouped[:].rearrange("p c t -> p (c t)"),
+            )
+
+        def turn_left():
+            words = al_left[:].bitcast(F32)
+            bank = psum_misc.tile([P, 2, 2, P], F32, name="bank", tag="misc")
+            for e in range(2):
+                nc.tensor.transpose(bank[:, 0, e, :], words[:, e : N // 2 : 2], ident[:])
+            lgrouped = keep.tile([P, P, PACK], BF16, name="lgrouped", align_bytes=64)
+            nc.scalar.copy(out=lgrouped[:].bitcast(F32), in_=bank[:, 0].rearrange("p e m -> p m e"))
+            return lgrouped
+
+        def stage1(h, a, rhs, rhs_scale, bank):
+            nc.tensor.matmul_mx(
+                out=bank,
+                lhsT=mw[:, h, a, :].bitcast(FP4X4),
+                lhsT_scale=ms[:, h, a, :],
+                rhs=rhs.bitcast(FP8X4),
+                rhs_scale=rhs_scale,
+                start=True,
+                stop=True,
+            )
+
+        f_t, a_t, x_t, d_t, dc_t, ds_t = {}, {}, {}, {}, {}, {}
+        eta_t, halo_t, up_t, r_t, rb_t, div_t = {}, {}, {}, {}, {}, {}
+
+        def m1(c, h, a):
+            eta = psum_eta.tile([P, CELLS], F32, name="eta")
+            stage1(h, a, codes[:, c, :], scales[:, c, :], eta[:])
+            eta_t[c, h, a] = eta
+
+        def m1_halo(c, h):
+            nxt = (c + 1) % CHUNKS
+            halo = psum_misc.tile([P, PACK, P], F32, name="halo", tag="misc")
+            for a in range(PACK):
+                stage1(h, a, codes[:, nxt, 0:P], scales[:, nxt, 0:P], halo[:, a, :])
+            halo_t[c, h] = halo
+
+        def new_f(c, h):
+            if (c, h) not in f_t:
+                f = work3.tile([P, PACK, PACK, PITCH], F32, name="f")
+                f_t[c, h] = f
+
+        def exp(c, h, a):
+            new_f(c, h)
+            nc.scalar.activation(
+                out=f_t[c, h][:, a, :, 0:P],
+                in_=eta_t[c, h, a][:].rearrange("p (t m) -> p t m", t=PACK),
+                func=ACT.Exp,
+            )
+
+        def exp_halo(c, h):
+            new_f(c, h)
+            nc.scalar.activation(out=f_t[c, h][:, :, 0, P : P + 1], in_=halo_t[c, h][:, :, 0:1], func=ACT.Exp)
+
+        def forward(c, h, a):
+            if (c, h) not in a_t:
+                fw = work3.tile([P, PACK, PACK, P], F32, name="fw")
+                a_t[c, h] = fw
+            j = h * PACK + a
+            nc.scalar.activation(
+                out=a_t[c, h][:, a], in_=f_t[c, h][:, a, :, 0:P], func=ACT.Copy, scale=wpos[:, j : j + 1]
+            )
+
+        def flux(c, h, a):
+            if (c, h) not in x_t:
+                x = work4.tile([P, PACK, PACK, PITCH], F32, name="x")
+                x_t[c, h] = x
+            j = h * PACK + a
+            f, fw, x = f_t[c, h], a_t[c, h], x_t[c, h]
+            nc.vector.scalar_tensor_tensor(
+                out=x[:, a, 0:3, LEAD : LEAD + P], in0=f[:, a, 1:4, 0:P], scalar=wneg[:, j : j + 1],
+                in1=fw[:, a, 0:3, :], op0=ALU.mult, op1=ALU.add,
+            )
+            nc.vector.scalar_tensor_tensor(
+                out=x[:, a, 3, LEAD : LEAD + P], in0=f[:, a, 0, 1 : P + 1], scalar=wneg[:, j : j + 1],
+                in1=fw[:, a, 3, :], op0=ALU.mult, op1=ALU.add,
+            )
+
+        fl_t = {}
+
+        def assist(c, h, a):
+            if (c, h) not in x_t:
+                x = work4.tile([P, PACK, PACK, PITCH], F32, name="x")
+                x_t[c, h] = x
+            f = f_t[c, h]
+            bank = psum_misc.tile([P, PACK, P], F32, name="fl", tag="misc")
+            pos, neg = diag[h, a]
+            nc.tensor.matmul(bank[:, 0:3, :], pos[:], f[:, a, 0:3, 0:P], start=True, stop=False)
+            nc.tensor.matmul(bank[:, 0:3, :], neg[:], f[:, a, 1:4, 0:P], start=False, stop=True)
+            nc.tensor.matmul(bank[:, 3, :], neg[:], f[:, a, 0, 1 : P + 1], start=True, stop=False)
+            nc.tensor.matmul(bank[:, 3, :], pos[:], f[:, a, 3, 0:P], start=False, stop=True)
+            fl_t[c, h, a] = bank
+
+        def assist_out(c, h, a):
+            nc.scalar.copy(out=x_t[c, h][:, a, :, LEAD : LEAD + P], in_=fl_t[c, h, a][:])
+
+        def left_flux(c, h):
+            dst = x_t[c, h][:, :, 3, LEAD - 1 : LEAD]
+            if c > 0:
+                nc.gpsimd.tensor_copy(out=dst, in_=x_t[c - 1, h][:, :, 3, LEAD + P - 1 : LEAD + P])
+                return
+            cols = slice(h * PACK, (h + 1) * PACK)
+            nc.gpsimd.tensor_tensor(out=l_pos[:, h], in0=f_last[:, h], in1=wpos[:, cols], op=ALU.mult)
+            nc.gpsimd.tensor_tensor(
+                out=l_neg[:, h].unsqueeze(2), in0=f_t[0, h][:, :, 0, 0:1], in1=wneg[:, cols].unsqueeze(2), op=ALU.mult
+            )
+            nc.gpsimd.tensor_tensor(out=dst, in0=l_pos[:, h].unsqueeze(2), in1=l_neg[:, h].unsqueeze(2), op=ALU.add)
+
+        def diff_rest(c, h):
+            d = work3.tile([P, PACK, P, PACK], BF16, name="d", align_bytes=64)
+            d_t[c, h] = d
+            x = x_t[c, h]
+            nc.vector.tensor_tensor(
+                out=d[:, 1:4],
+                in0=x[:, :, 1:4, LEAD : LEAD + P].rearrange("p a t m -> p t m a"),
+                in1=x[:, :, 0:3, LEAD : LEAD + P].rearrange("p a t m -> p t m a"),
+                op=ALU.subtract,
+            )
+
+        def diff_first(c, h):
+            x = x_t[c, h]
+            nc.vector.tensor_tensor(
+                out=d_t[c, h][:, 0],
+                in0=x[:, :, 0, LEAD : LEAD + P].rearrange("p a m -> p m a"),
+                in1=x[:, :, 3, LEAD - 1 : LEAD + P - 1].rearrange("p a m -> p m a"),
+                op=ALU.subtract,
+            )
+
+        def quant_d(c, h):
+            dc = work4.tile([P, CELLS], U32, name="dc", align_bytes=64)
+            ds = work4.tile([P, CELLS], U8, name="ds", align_bytes=64)
+            nc.vector.quantize_mx(
+                out=dc[:].bitcast(FP8X4), scales=ds[:], in_=d_t[c, h][:].rearrange("p t m a -> p (t m a)")
+            )
+            dc_t[c, h], ds_t[c, h] = dc, ds
+
+        def m2(c, t):
+            div = psum_div.tile([P, N], F32, name="div")
+            cols = slice(t * P, (t + 1) * P)
+            for h in range(PASSES):
+                nc.tensor.matmul_mx(
+                    out=div[:],
+                    lhsT=dc_t[c, h][:, cols].bitcast(FP8X4),
+                    lhsT_scale=ds_t[c, h][:, cols],
+                    rhs=pw[:, h, :].bitcast(FP4X4),
+                    rhs_scale=ps[:, h, :],
+                    start=(h == 0),
+                    stop=(h == PASSES - 1),
+                )
+            div_t[c, t] = div
+
+        def scaled_u(c, t):
+            up = single.tile([P, N], F32, name="up", tag="up%d" % t)
+            up_t[c, t] = up
+            j = c * PACK + t
+            nc.gpsimd.tensor_scalar(
+                out=up[:], in0=ut[c][:, t], scalar1=rden[:, j : j + 1], scalar2=0.0, op0=ALU.mult, op1=ALU.add
+            )
+
+        def update(c, t):
+            if t == 0:
+                r = work.tile([P, PACK, N], F32, name="r")
+                r_t[c] = r
+            j = c * PACK + t
+            nc.vector.scalar_tensor_tensor(
+                out=r_t[c][:, t], in0=div_t[c, t][:], scalar=rneg[:, j : j + 1], in1=up_t[c, t][:],
+                op0=ALU.mult, op1=ALU.add,
+            )
+            nc.sync.dma_start(out=out_rows[c, :, t, :], in_=r_t[c][:, t])
+
+        def round_half(c, half):
+            rb = work4.tile([P, N // 2, PACK], BF16, name="rb", align_bytes=64)
+            rb_t[c, half] = rb
+            src = r_t[c][:, :, half * N // 2 : (half + 1) * N // 2].rearrange("p t n -> p n t")
+            if half == 0 and c == CHUNKS - 1:
+                nc.vector.tensor_copy(out=rb[:], in_=src)
+            else:
+                nc.scalar.copy(out=rb[:], in_=src)
+
+        pl_t = {}
+
+        def planes_half(c, half):
+            if half == 0:
+                pc = work.tile([P, N], U32, name="pc", align_bytes=64)
+                pq = work.tile([P, N], U8, name="pq", align_bytes=64)
+                pl_t[c] = (pc, pq)
+            pc, pq = pl_t[c]
+            cols = slice(half * N // 2, (half + 1) * N // 2)
+            nc.vector.quantize_mx(
+                out=pc[:, cols].bitcast(FP8X4), scales=pq[:, cols],
+                in_=rb_t[c, half][:].rearrange("p n t -> p (n t)"),
+            )
+            if half == 1:
+                nc.sync.dma_start(out=out_1[c].rearrange("p m t -> p (m t)").bitcast(I32), in_=pc[:].bitcast(I32))
+                for quad in range(4):
+                    nc.sync.dma_start(
+                        out=out_2[c, 4 * quad : 4 * quad + 4, :].bitcast(I32),
+                        in_=pq[32 * quad : 32 * quad + 4, :].bitcast(I32),
+                    )
+
+        w_view = w_sb[:, :, 0:PACK]
+        nc.vector.tensor_scalar(out=wpos[:].rearrange("p (h a) -> p h a", a=PACK), in0=w_view, scalar1=0.0, scalar2=None, op0=ALU.max)
+        nc.vector.tensor_scalar(out=wneg[:].rearrange("p (h a) -> p h a", a=PACK), in0=w_view, scalar1=0.0, scalar2=None, op0=ALU.min)
+        g00 = turn_half(0, 0, "s")
+        g01 = turn_half(0, 1, "s")
+        permute_m(0)
+        quant_half(0, 0, g00)
+        quant_half(0, 1, g01)
+        lg = turn_left()
+        g10 = turn_half(1, 0, "s")
+        g11 = turn_half(1, 1, "v")
+        quant_half(1, 0, g10)
+        quant_half(1, 1, g11)
+        permute_m(1)
+        nc.vector.quantize_mx(out=lcodes[:].bitcast(FP8X4), scales=lscales[:], in_=lg[:].rearrange("p c t -> p (c t)"))
+        s_view = s_sb[:, :, 0:PACK]
+        nc.vector.tensor_scalar(out=s1[:].rearrange("p (c t) -> p c t", t=PACK), in0=s_view, scalar1=1.0, scalar2=None, op0=ALU.add)
+        nc.vector.reciprocal(out=rden[:], in_=s1[:])
+        nc.vector.tensor_scalar(out=rneg[:], in0=rden[:], scalar1=-0.5, scalar2=None, op0=ALU.mult)
+        diag = {}
+        for h in range(PASSES):
+            for a in ASSIST[h]:
+                pair = []
+                for sign, col in (("pos", wpos), ("neg", wneg)):
+                    dg = keep.tile([P, P], F32, name="dg", tag="dg_%s_%d_%d" % (sign, h, a))
+                    j = h * PACK + a
+                    nc.gpsimd.tensor_scalar(
+                        out=dg[:], in0=ident[:], scalar1=col[:, j : j + 1], scalar2=0.0, op0=ALU.mult, op1=ALU.add
+                    )
+                    pair.append(dg)
+                diag[h, a] = pair
+
+        def left_pe(h):
+            left = psum_misc.tile([P, PACK, P], F32, name="halo", tag="misc")
+            for a in range(PACK):
+                stage1(h, a, lcodes[:], lscales[:], left[:, a, :])
+            nc.scalar.activation(out=f_last[:, h].unsqueeze(2), in_=left[:, :, P - 1 : P], func=ACT.Exp)
+
+        free = [[a for a in range(PACK) if a not in ASSIST[h]] for h in range(PASSES)]
+        order = [list(ASSIST[h]) + free[h] for h in range(PASSES)]
+
+        def front(c, h):
+            helped, own, seq = ASSIST[h], free[h], order[h]
+            exp(c, h, seq[0])
+            exp_halo(c, h)
+            if helped:
+                assist(c, h, helped[0])
+            exp(c, h, seq[1])
+            if len(helped) > 1:
+                assist(c, h, helped[1])
+            pending = []
+            for i in range(2, PACK):
+                exp(c, h, seq[i])
+                if seq[i - 1] in own:
+                    forward(c, h, seq[i - 1])
+            forward(c, h, seq[PACK - 1])
+            for a in helped:
+                assist_out(c, h, a)
+
+        for t in range(PACK):
+            scaled_u(0, t)
+        for c in range(CHUNKS):
+            if c == 0:
+                m1(c, 0, order[0][0])
+                m1(c, 0, order[0][1])
+            m1_halo(c, 0)
+            m1(c, 0, order[0][2])
+            m1(c, 0, order[0][3])
+            front(c, 0)
+            if c == 0:
+                left_pe(0)
+                left_pe(1)
+            grouped = []
+            if c + 2 < CHUNKS:
+                grouped = [turn_half(c + 2, 0, "s"), turn_half(c + 2, 1, "s")]
+            m1(c, 1, order[1][0])
+            m1(c, 1, order[1][1])
+            m1_halo(c, 1)
+            flux(c, 0, free[0][0])
+            if c > 0:
+                quant_d(c - 1, 1)
+                for t in range(3):
+                    m2(c - 1, t)
+            for a in free[0][1:]:
+                flux(c, 0, a)
+            m1(c, 1, order[1][2])
+            left_flux(c, 0)
+            if c > 0:
+                update(c - 1, 0)
+                m2(c - 1, 3)
+            diff_rest(c, 0)
+            m1(c, 1, order[1][3])
+            diff_first(c, 0)
+            if c > 0:
+                scaled_u(c, 0)
+                for t in range(1, PACK):
+                    update(c - 1, t)
+                    scaled_u(c, t)
+            front(c, 1)
+            if c + 1 < CHUNKS:
+                m1(c + 1, 0, order[0][0])
+                m1(c + 1, 0, order[0][1])
+            if c > 0:
+                round_half(c - 1, 0)
+                round_half(c - 1, 1)
+            flux(c, 1, free[1][0])
+            quant_d(c, 0)
+            for half, g in enumerate(grouped):
+                quant_half(c + 2, half, g)
+            for a in free[1][1:]:
+                flux(c, 1, a)
+            left_flux(c, 1)
+            if c > 1:
+                planes_half(c - 2, 0)
+                planes_half(c - 2, 1)
+            diff_rest(c, 1)
+            diff_first(c, 1)
+
+        c = CHUNKS - 1
+        planes_half(c - 1, 0)
+        quant_d(c, 1)
+        planes_half(c - 1, 1)
+        for t in range(PACK):
+            m2(c, t)
+            update(c, t)
+        round_half(c, 0)
+        round_half(c, 1)
+        planes_half(c, 0)
+        planes_half(c, 1)

@@ -40,7 +40,6 @@ def tile_entropyclosuremomentkineticupwindstep_x2_kernel(
         psum_eta = ctx.enter_context(tc.psum_pool(name="psum_eta", bufs=2))
         psum_misc = ctx.enter_context(tc.psum_pool(name="psum_misc", bufs=3))
         psum_div = ctx.enter_context(tc.psum_pool(name="psum_div", bufs=3))
-        single = ctx.enter_context(tc.tile_pool(name="single", bufs=1))
         ctx.enter_context(tc.manual_schedule())
 
         ident = keep.tile([P, P], F32, name="ident")
@@ -236,25 +235,26 @@ def tile_entropyclosuremomentkineticupwindstep_x2_kernel(
             )
             nc.gpsimd.tensor_tensor(out=dst, in0=l_pos[:, h].unsqueeze(2), in1=l_neg[:, h].unsqueeze(2), op=ALU.add)
 
-        def diff_rest(c, h):
-            d = work3.tile([P, PACK, P, PACK], BF16, name="d", align_bytes=64)
-            d_t[c, h] = d
+        def diff(c, h, t):
+            if t == 1:
+                d = work3.tile([P, PACK, P, PACK], BF16, name="d", align_bytes=64)
+                d_t[c, h] = d
             x = x_t[c, h]
+            back = x[:, :, t - 1, LEAD : LEAD + P] if t > 0 else x[:, :, 3, LEAD - 1 : LEAD + P - 1]
+            runs = "p a (g i) -> p g a i"
             nc.vector.tensor_tensor(
-                out=d[:, 1:4],
-                in0=x[:, :, 1:4, LEAD : LEAD + P].rearrange("p a t m -> p t m a"),
-                in1=x[:, :, 0:3, LEAD : LEAD + P].rearrange("p a t m -> p t m a"),
+                out=d_t[c, h][:, t].rearrange("p (g i) a -> p g a i", i=4),
+                in0=x[:, :, t, LEAD : LEAD + P].rearrange(runs, i=4),
+                in1=back.rearrange(runs, i=4),
                 op=ALU.subtract,
             )
 
+        def diff_rest(c, h):
+            for t in range(1, PACK):
+                diff(c, h, t)
+
         def diff_first(c, h):
-            x = x_t[c, h]
-            nc.vector.tensor_tensor(
-                out=d_t[c, h][:, 0],
-                in0=x[:, :, 0, LEAD : LEAD + P].rearrange("p a m -> p m a"),
-                in1=x[:, :, 3, LEAD - 1 : LEAD + P - 1].rearrange("p a m -> p m a"),
-                op=ALU.subtract,
-            )
+            diff(c, h, 0)
 
         def quant_d(c, h):
             dc = work4.tile([P, CELLS], U32, name="dc", align_bytes=64)
@@ -280,12 +280,10 @@ def tile_entropyclosuremomentkineticupwindstep_x2_kernel(
             div_t[c, t] = div
 
         def scaled_u(c, t):
-            up = single.tile([P, N], F32, name="up", tag="up%d" % t)
+            up = work.tile([P, N], F32, name="up", tag="up%d" % t)
             up_t[c, t] = up
             j = c * PACK + t
-            nc.gpsimd.tensor_scalar(
-                out=up[:], in0=ut[c][:, t], scalar1=rden[:, j : j + 1], scalar2=0.0, op0=ALU.mult, op1=ALU.add
-            )
+            nc.scalar.activation(out=up[:], in_=ut[c][:, t], func=ACT.Copy, scale=rden[:, j : j + 1])
 
         def update(c, t):
             if t == 0:
@@ -387,8 +385,6 @@ def tile_entropyclosuremomentkineticupwindstep_x2_kernel(
             for a in helped:
                 assist_out(c, h, a)
 
-        for t in range(PACK):
-            scaled_u(0, t)
         for c in range(CHUNKS):
             if c == 0:
                 m1(c, 0, order[0][0])
@@ -422,14 +418,16 @@ def tile_entropyclosuremomentkineticupwindstep_x2_kernel(
             m1(c, 1, order[1][3])
             diff_first(c, 0)
             if c > 0:
-                scaled_u(c, 0)
                 for t in range(1, PACK):
                     update(c - 1, t)
-                    scaled_u(c, t)
+            scaled_u(c, 0)
+            scaled_u(c, 1)
             front(c, 1)
             if c + 1 < CHUNKS:
                 m1(c + 1, 0, order[0][0])
                 m1(c + 1, 0, order[0][1])
+            scaled_u(c, 2)
+            scaled_u(c, 3)
             if c > 0:
                 round_half(c - 1, 0)
                 round_half(c - 1, 1)

@@ -23,7 +23,7 @@ CELLS = P * PACK
 CHUNKS = X // CELLS
 PASSES = Q // (P * PACK)
 PITCH = 136
-ASSIST = {0: (0,), 1: (0,)}
+ASSIST = {0: (), 1: ()}
 LEAD = 8
 
 
@@ -376,7 +376,8 @@ def tile_entropyclosuremomentkineticupwindstep_x2_kernel(
             exp(c, h, seq[1])
             if len(helped) > 1:
                 assist(c, h, helped[1])
-            pending = []
+            if not helped:
+                forward(c, h, seq[0])
             for i in range(2, PACK):
                 exp(c, h, seq[i])
                 if seq[i - 1] in own:

@@ -23,8 +23,13 @@ CELLS = P * PACK
 CHUNKS = X // CELLS
 PASSES = Q // (P * PACK)
 PITCH = 136
-ASSIST = {0: (), 1: ()}
 LEAD = 8
+HALF = N // 2
+POOL_U = 3
+
+
+def assisted(c, h):
+    return h == 1
 
 
 def tile_entropyclosuremomentkineticupwindstep_x2_kernel(
@@ -35,6 +40,7 @@ def tile_entropyclosuremomentkineticupwindstep_x2_kernel(
         keep = ctx.enter_context(tc.tile_pool(name="keep", bufs=1))
         load = ctx.enter_context(tc.tile_pool(name="load", bufs=CHUNKS))
         work = ctx.enter_context(tc.tile_pool(name="work", bufs=2))
+        single = ctx.enter_context(tc.tile_pool(name="single", bufs=1))
         work3 = ctx.enter_context(tc.tile_pool(name="work3", bufs=3))
         work4 = ctx.enter_context(tc.tile_pool(name="work4", bufs=4))
         psum_eta = ctx.enter_context(tc.psum_pool(name="psum_eta", bufs=2))
@@ -100,43 +106,47 @@ def tile_entropyclosuremomentkineticupwindstep_x2_kernel(
             nc.sync.dma_start(out=ut[c - 1][:], in_=u_rows[c - 1])
         nc.sync.dma_start(out=ut[CHUNKS - 1][:], in_=u_rows[CHUNKS - 1])
 
-        def permute_m(h):
+        def permute_m(h, first, count):
+            pick = slice(first, first + count)
             raw = m_raw[:, h * N * 2 : (h + 1) * N * 2].rearrange("p (m a b) -> p a m b", a=PACK, b=2)
-            nc.vector.tensor_copy(out=mw[:, h].rearrange("p a (m b) -> p a m b", b=2), in_=raw)
+            nc.vector.tensor_copy(
+                out=mw[:, h, pick].rearrange("p a (m b) -> p a m b", b=2), in_=raw[:, pick]
+            )
             plane = m_plane[:, h * N : (h + 1) * N].rearrange("p (m a) -> p a m", a=PACK)
-            nc.vector.tensor_copy(out=ms[:, h], in_=plane)
+            nc.vector.tensor_copy(out=ms[:, h, pick], in_=plane[:, pick])
 
-        def turn_half(c, half, engine):
+        grouped_t = {}
+
+        def turn(c, half):
             words = al[c][:].bitcast(F32)
             bank = psum_misc.tile([P, 2, 2, P], F32, name="bank", tag="misc")
             for t in range(2):
                 for e in range(2):
                     nc.tensor.transpose(bank[:, t, e, :], words[:, 2 * half + t, e : N // 2 : 2], ident[:])
-            grouped = work4.tile([P, 2 * P, PACK], BF16, name="grouped", align_bytes=64)
-            dst = grouped[:].bitcast(F32).rearrange("p (t m) e -> p t m e", t=2)
-            src = bank[:].rearrange("p t e m -> p t m e")
-            if engine == "v":
-                nc.vector.tensor_copy(out=dst, in_=src)
-            else:
-                nc.scalar.copy(out=dst, in_=src)
-            return grouped
+            if half == 0:
+                grouped = work.tile([P, 2, 2 * P, PACK], BF16, name="grouped", align_bytes=64)
+                grouped_t[c] = grouped
+            nc.scalar.copy(
+                out=grouped_t[c][:, half].bitcast(F32).rearrange("p (t m) e -> p t m e", t=2),
+                in_=bank[:].rearrange("p t e m -> p t m e"),
+            )
 
-        def quant_half(c, half, grouped):
-            cols = slice(half * 2 * P, (half + 1) * 2 * P)
+        def quant_alpha(c, first=0, count=2):
+            cols = slice(first * 2 * P, (first + count) * 2 * P)
             nc.vector.quantize_mx(
                 out=codes[:, c, cols].bitcast(FP8X4),
                 scales=scales[:, c, cols],
-                in_=grouped[:].rearrange("p c t -> p (c t)"),
+                in_=grouped_t[c][:, first : first + count].rearrange("p s c t -> p (s c t)"),
             )
+
+        lgrouped = keep.tile([P, P, PACK], BF16, name="lgrouped", align_bytes=64)
 
         def turn_left():
             words = al_left[:].bitcast(F32)
             bank = psum_misc.tile([P, 2, 2, P], F32, name="bank", tag="misc")
             for e in range(2):
                 nc.tensor.transpose(bank[:, 0, e, :], words[:, e : N // 2 : 2], ident[:])
-            lgrouped = keep.tile([P, P, PACK], BF16, name="lgrouped", align_bytes=64)
             nc.scalar.copy(out=lgrouped[:].bitcast(F32), in_=bank[:, 0].rearrange("p e m -> p m e"))
-            return lgrouped
 
         def stage1(h, a, rhs, rhs_scale, bank):
             nc.tensor.matmul_mx(
@@ -150,7 +160,7 @@ def tile_entropyclosuremomentkineticupwindstep_x2_kernel(
             )
 
         f_t, a_t, x_t, d_t, dc_t, ds_t = {}, {}, {}, {}, {}, {}
-        eta_t, halo_t, up_t, r_t, rb_t, div_t = {}, {}, {}, {}, {}, {}
+        eta_t, halo_t, up_t, r_t, rb_t, div_t, pl_t = {}, {}, {}, {}, {}, {}, {}
 
         def m1(c, h, a):
             eta = psum_eta.tile([P, CELLS], F32, name="eta")
@@ -164,13 +174,10 @@ def tile_entropyclosuremomentkineticupwindstep_x2_kernel(
                 stage1(h, a, codes[:, nxt, 0:P], scales[:, nxt, 0:P], halo[:, a, :])
             halo_t[c, h] = halo
 
-        def new_f(c, h):
-            if (c, h) not in f_t:
+        def exp(c, h, a):
+            if a == 0:
                 f = work3.tile([P, PACK, PACK, PITCH], F32, name="f")
                 f_t[c, h] = f
-
-        def exp(c, h, a):
-            new_f(c, h)
             nc.scalar.activation(
                 out=f_t[c, h][:, a, :, 0:P],
                 in_=eta_t[c, h, a][:].rearrange("p (t m) -> p t m", t=PACK),
@@ -178,10 +185,11 @@ def tile_entropyclosuremomentkineticupwindstep_x2_kernel(
             )
 
         def exp_halo(c, h):
-            new_f(c, h)
             nc.scalar.activation(out=f_t[c, h][:, :, 0, P : P + 1], in_=halo_t[c, h][:, :, 0:1], func=ACT.Exp)
 
         def forward(c, h, a):
+            if a == 0 and assisted(c, h):
+                return
             if (c, h) not in a_t:
                 fw = work3.tile([P, PACK, PACK, P], F32, name="fw")
                 a_t[c, h] = fw
@@ -190,43 +198,53 @@ def tile_entropyclosuremomentkineticupwindstep_x2_kernel(
                 out=a_t[c, h][:, a], in_=f_t[c, h][:, a, :, 0:P], func=ACT.Copy, scale=wpos[:, j : j + 1]
             )
 
-        def flux(c, h, a):
+        S3, S0 = LEAD, LEAD + P
+
+        def flux_wrap(c, h, a):
+            if a == 0 and assisted(c, h):
+                return
+            j = h * PACK + a
+            nc.vector.scalar_tensor_tensor(
+                out=x_t[c, h][:, a, S3 : S3 + P], in0=f_t[c, h][:, a, 0, 1 : P + 1], scalar=wneg[:, j : j + 1],
+                in1=a_t[c, h][:, a, 3, :], op0=ALU.mult, op1=ALU.add,
+            )
+
+        def x_new(c, h):
             if (c, h) not in x_t:
-                x = work4.tile([P, PACK, PACK, PITCH], F32, name="x")
+                x = work4.tile([P, PACK, LEAD + CELLS], F32, name="x")
                 x_t[c, h] = x
+
+        def flux(c, h, a):
+            if a == 0 and assisted(c, h):
+                return
+            x_new(c, h)
             j = h * PACK + a
             f, fw, x = f_t[c, h], a_t[c, h], x_t[c, h]
             nc.vector.scalar_tensor_tensor(
-                out=x[:, a, 0:3, LEAD : LEAD + P], in0=f[:, a, 1:4, 0:P], scalar=wneg[:, j : j + 1],
-                in1=fw[:, a, 0:3, :], op0=ALU.mult, op1=ALU.add,
-            )
-            nc.vector.scalar_tensor_tensor(
-                out=x[:, a, 3, LEAD : LEAD + P], in0=f[:, a, 0, 1 : P + 1], scalar=wneg[:, j : j + 1],
-                in1=fw[:, a, 3, :], op0=ALU.mult, op1=ALU.add,
+                out=x[:, a, S0 : S0 + 3 * P].rearrange("p (t m) -> p t m", t=3), in0=f[:, a, 1:4, 0:P],
+                scalar=wneg[:, j : j + 1], in1=fw[:, a, 0:3, :], op0=ALU.mult, op1=ALU.add,
             )
 
         fl_t = {}
 
         def assist(c, h, a):
-            if (c, h) not in x_t:
-                x = work4.tile([P, PACK, PACK, PITCH], F32, name="x")
-                x_t[c, h] = x
             f = f_t[c, h]
             bank = psum_misc.tile([P, PACK, P], F32, name="fl", tag="misc")
-            pos, neg = diag[h, a]
-            nc.tensor.matmul(bank[:, 0:3, :], pos[:], f[:, a, 0:3, 0:P], start=True, stop=False)
-            nc.tensor.matmul(bank[:, 0:3, :], neg[:], f[:, a, 1:4, 0:P], start=False, stop=True)
-            nc.tensor.matmul(bank[:, 3, :], neg[:], f[:, a, 0, 1 : P + 1], start=True, stop=False)
-            nc.tensor.matmul(bank[:, 3, :], pos[:], f[:, a, 3, 0:P], start=False, stop=True)
-            fl_t[c, h, a] = bank
+            pos, neg = diag[h]
+            nc.tensor.matmul(bank[:, 1:4, :], pos[:], f[:, a, 0:3, 0:P], start=True, stop=False)
+            nc.tensor.matmul(bank[:, 1:4, :], neg[:], f[:, a, 1:4, 0:P], start=False, stop=True)
+            nc.tensor.matmul(bank[:, 0, :], neg[:], f[:, a, 0, 1 : P + 1], start=True, stop=False)
+            nc.tensor.matmul(bank[:, 0, :], pos[:], f[:, a, 3, 0:P], start=False, stop=True)
+            fl_t[c, h] = bank
 
         def assist_out(c, h, a):
-            nc.scalar.copy(out=x_t[c, h][:, a, :, LEAD : LEAD + P], in_=fl_t[c, h, a][:])
+            x_new(c, h)
+            nc.scalar.copy(out=x_t[c, h][:, a, LEAD : LEAD + CELLS], in_=fl_t[c, h][:].rearrange("p t m -> p (t m)"))
 
         def left_flux(c, h):
-            dst = x_t[c, h][:, :, 3, LEAD - 1 : LEAD]
+            dst = x_t[c, h][:, :, LEAD - 1 : LEAD]
             if c > 0:
-                nc.gpsimd.tensor_copy(out=dst, in_=x_t[c - 1, h][:, :, 3, LEAD + P - 1 : LEAD + P])
+                nc.gpsimd.tensor_copy(out=dst, in_=x_t[c - 1, h][:, :, S3 + P - 1 : S3 + P])
                 return
             cols = slice(h * PACK, (h + 1) * PACK)
             nc.gpsimd.tensor_tensor(out=l_pos[:, h], in0=f_last[:, h], in1=wpos[:, cols], op=ALU.mult)
@@ -235,34 +253,33 @@ def tile_entropyclosuremomentkineticupwindstep_x2_kernel(
             )
             nc.gpsimd.tensor_tensor(out=dst, in0=l_pos[:, h].unsqueeze(2), in1=l_neg[:, h].unsqueeze(2), op=ALU.add)
 
-        def diff(c, h, t):
-            if t == 1:
-                d = work3.tile([P, PACK, P, PACK], BF16, name="d", align_bytes=64)
+        def diff(c, h, t, count=1):
+            if (c, h) not in d_t:
+                d = work3.tile([P, CELLS, PACK], BF16, name="d", align_bytes=64)
                 d_t[c, h] = d
             x = x_t[c, h]
-            back = x[:, :, t - 1, LEAD : LEAD + P] if t > 0 else x[:, :, 3, LEAD - 1 : LEAD + P - 1]
+            here = S0 + t * P if t < 3 else S3
+            back = {0: S3 - 1, 1: S0, 3: S0 + 2 * P}[t]
+            width = count * P
             runs = "p a (g i) -> p g a i"
+            run = 8 if t == 0 else 4
             nc.vector.tensor_tensor(
-                out=d_t[c, h][:, t].rearrange("p (g i) a -> p g a i", i=4),
-                in0=x[:, :, t, LEAD : LEAD + P].rearrange(runs, i=4),
-                in1=back.rearrange(runs, i=4),
+                out=d_t[c, h][:, t * P : t * P + width].rearrange("p (g i) a -> p g a i", i=run),
+                in0=x[:, :, here : here + width].rearrange(runs, i=run),
+                in1=x[:, :, back : back + width].rearrange(runs, i=run),
                 op=ALU.subtract,
             )
 
-        def diff_rest(c, h):
-            for t in range(1, PACK):
-                diff(c, h, t)
-
-        def diff_first(c, h):
-            diff(c, h, 0)
-
-        def quant_d(c, h):
-            dc = work4.tile([P, CELLS], U32, name="dc", align_bytes=64)
-            ds = work4.tile([P, CELLS], U8, name="ds", align_bytes=64)
+        def quant_d(c, h, first=0, count=PACK):
+            if first == 0:
+                dc = work4.tile([P, CELLS], U32, name="dc", align_bytes=64)
+                ds = work4.tile([P, CELLS], U8, name="ds", align_bytes=64)
+                dc_t[c, h], ds_t[c, h] = dc, ds
+            cols = slice(first * P, (first + count) * P)
             nc.vector.quantize_mx(
-                out=dc[:].bitcast(FP8X4), scales=ds[:], in_=d_t[c, h][:].rearrange("p t m a -> p (t m a)")
+                out=dc_t[c, h][:, cols].bitcast(FP8X4), scales=ds_t[c, h][:, cols],
+                in_=d_t[c, h][:, cols].rearrange("p x a -> p (x a)"),
             )
-            dc_t[c, h], ds_t[c, h] = dc, ds
 
         def m2(c, t):
             div = psum_div.tile([P, N], F32, name="div")
@@ -280,10 +297,16 @@ def tile_entropyclosuremomentkineticupwindstep_x2_kernel(
             div_t[c, t] = div
 
         def scaled_u(c, t):
-            up = work.tile([P, N], F32, name="up", tag="up%d" % t)
-            up_t[c, t] = up
             j = c * PACK + t
-            nc.scalar.activation(out=up[:], in_=ut[c][:, t], func=ACT.Copy, scale=rden[:, j : j + 1])
+            if t < POOL_U:
+                up = single.tile([P, N], F32, name="up", tag="up%d" % t)
+                nc.gpsimd.tensor_scalar(
+                    out=up[:], in0=ut[c][:, t], scalar1=rden[:, j : j + 1], scalar2=0.0, op0=ALU.mult, op1=ALU.add
+                )
+            else:
+                up = work.tile([P, N], F32, name="up", tag="up%d" % t)
+                nc.scalar.activation(out=up[:], in_=ut[c][:, t], func=ACT.Copy, scale=rden[:, j : j + 1])
+            up_t[c, t] = up
 
         def update(c, t):
             if t == 0:
@@ -297,29 +320,32 @@ def tile_entropyclosuremomentkineticupwindstep_x2_kernel(
             nc.sync.dma_start(out=out_rows[c, :, t, :], in_=r_t[c][:, t])
 
         def round_half(c, half):
-            rb = work4.tile([P, N // 2, PACK], BF16, name="rb", align_bytes=64)
-            rb_t[c, half] = rb
-            src = r_t[c][:, :, half * N // 2 : (half + 1) * N // 2].rearrange("p t n -> p n t")
-            if half == 0 and c == CHUNKS - 1:
-                nc.vector.tensor_copy(out=rb[:], in_=src)
-            else:
-                nc.scalar.copy(out=rb[:], in_=src)
-
-        pl_t = {}
-
-        def planes_half(c, half):
             if half == 0:
+                rb = work.tile([P, N, PACK], BF16, name="rb", align_bytes=64)
+                rb_t[c] = rb
+            cols = slice(half * HALF, (half + 1) * HALF)
+            src = r_t[c][:, :, cols].rearrange("p t (g i) -> p g t i", i=4)
+            dst = rb_t[c][:, cols].rearrange("p (g i) t -> p g t i", i=4)
+            if half == 0 and c == CHUNKS - 1:
+                nc.vector.tensor_copy(out=dst, in_=src)
+            else:
+                nc.scalar.copy(out=dst, in_=src)
+
+        def planes(c, first=0, count=2):
+            if first == 0:
                 pc = work.tile([P, N], U32, name="pc", align_bytes=64)
                 pq = work.tile([P, N], U8, name="pq", align_bytes=64)
                 pl_t[c] = (pc, pq)
             pc, pq = pl_t[c]
-            cols = slice(half * N // 2, (half + 1) * N // 2)
+            cols = slice(first * HALF, (first + count) * HALF)
             nc.vector.quantize_mx(
                 out=pc[:, cols].bitcast(FP8X4), scales=pq[:, cols],
-                in_=rb_t[c, half][:].rearrange("p n t -> p (n t)"),
+                in_=rb_t[c][:, cols].rearrange("p n t -> p (n t)"),
             )
-            if half == 1:
-                nc.sync.dma_start(out=out_1[c].rearrange("p m t -> p (m t)").bitcast(I32), in_=pc[:].bitcast(I32))
+            nc.sync.dma_start(
+                out=out_1[c, :, cols, :].rearrange("p m t -> p (m t)").bitcast(I32), in_=pc[:, cols].bitcast(I32)
+            )
+            if first + count == 2:
                 for quad in range(4):
                     nc.sync.dma_start(
                         out=out_2[c, 4 * quad : 4 * quad + 4, :].bitcast(I32),
@@ -329,130 +355,156 @@ def tile_entropyclosuremomentkineticupwindstep_x2_kernel(
         w_view = w_sb[:, :, 0:PACK]
         nc.vector.tensor_scalar(out=wpos[:].rearrange("p (h a) -> p h a", a=PACK), in0=w_view, scalar1=0.0, scalar2=None, op0=ALU.max)
         nc.vector.tensor_scalar(out=wneg[:].rearrange("p (h a) -> p h a", a=PACK), in0=w_view, scalar1=0.0, scalar2=None, op0=ALU.min)
-        g00 = turn_half(0, 0, "s")
-        g01 = turn_half(0, 1, "s")
-        permute_m(0)
-        quant_half(0, 0, g00)
-        quant_half(0, 1, g01)
-        lg = turn_left()
-        g10 = turn_half(1, 0, "s")
-        g11 = turn_half(1, 1, "v")
-        quant_half(1, 0, g10)
-        quant_half(1, 1, g11)
-        permute_m(1)
-        nc.vector.quantize_mx(out=lcodes[:].bitcast(FP8X4), scales=lscales[:], in_=lg[:].rearrange("p c t -> p (c t)"))
         s_view = s_sb[:, :, 0:PACK]
+        turn(0, 0)
+        turn(0, 1)
+        permute_m(0, 0, 2)
+        quant_alpha(0, 0, 1)
+        quant_alpha(0, 1, 1)
+        turn_left()
+        for a in range(2):
+            m1(0, 0, a)
+        permute_m(0, 2, 2)
+        nc.vector.quantize_mx(out=lcodes[:].bitcast(FP8X4), scales=lscales[:], in_=lgrouped[:].rearrange("p c t -> p (c t)"))
         nc.vector.tensor_scalar(out=s1[:].rearrange("p (c t) -> p c t", t=PACK), in0=s_view, scalar1=1.0, scalar2=None, op0=ALU.add)
-        nc.vector.reciprocal(out=rden[:], in_=s1[:])
-        nc.vector.tensor_scalar(out=rneg[:], in0=rden[:], scalar1=-0.5, scalar2=None, op0=ALU.mult)
+        m1(0, 0, 2)
+
+        def second_half():
+            turn(1, 0)
+            turn(1, 1)
+            permute_m(1, 0, PACK)
+            nc.vector.reciprocal(out=rden[:], in_=s1[:])
+            quant_alpha(1)
+            m1_halo(0, 0)
+            nc.vector.tensor_scalar(out=rneg[:], in0=rden[:], scalar1=-0.5, scalar2=None, op0=ALU.mult)
+
+        def left_start():
+            for h in range(PASSES):
+                left = psum_misc.tile([P, PACK, P], F32, name="halo", tag="misc")
+                for a in range(PACK):
+                    stage1(h, a, lcodes[:], lscales[:], left[:, a, :])
+                nc.scalar.activation(out=f_last[:, h].unsqueeze(2), in_=left[:, :, P - 1 : P], func=ACT.Exp)
+            for t in range(POOL_U):
+                scaled_u(0, t)
+
+        pending = []
         diag = {}
         for h in range(PASSES):
-            for a in ASSIST[h]:
-                pair = []
-                for sign, col in (("pos", wpos), ("neg", wneg)):
-                    dg = keep.tile([P, P], F32, name="dg", tag="dg_%s_%d_%d" % (sign, h, a))
-                    j = h * PACK + a
-                    nc.gpsimd.tensor_scalar(
-                        out=dg[:], in0=ident[:], scalar1=col[:, j : j + 1], scalar2=0.0, op0=ALU.mult, op1=ALU.add
-                    )
-                    pair.append(dg)
-                diag[h, a] = pair
-
-        def left_pe(h):
-            left = psum_misc.tile([P, PACK, P], F32, name="halo", tag="misc")
-            for a in range(PACK):
-                stage1(h, a, lcodes[:], lscales[:], left[:, a, :])
-            nc.scalar.activation(out=f_last[:, h].unsqueeze(2), in_=left[:, :, P - 1 : P], func=ACT.Exp)
-
-        free = [[a for a in range(PACK) if a not in ASSIST[h]] for h in range(PASSES)]
-        order = [list(ASSIST[h]) + free[h] for h in range(PASSES)]
+            pair = []
+            for sign, col in (("pos", wpos), ("neg", wneg)):
+                dg = keep.tile([P, P], F32, name="dg", tag="dg_%s_%d" % (sign, h))
+                nc.gpsimd.tensor_scalar(
+                    out=dg[:], in0=ident[:], scalar1=col[:, h * PACK : h * PACK + 1], scalar2=0.0,
+                    op0=ALU.mult, op1=ALU.add,
+                )
+                pair.append(dg)
+            diag[h] = pair
 
         def front(c, h):
-            helped, own, seq = ASSIST[h], free[h], order[h]
-            exp(c, h, seq[0])
-            exp_halo(c, h)
-            if helped:
-                assist(c, h, helped[0])
-            exp(c, h, seq[1])
-            if len(helped) > 1:
-                assist(c, h, helped[1])
-            if not helped:
-                forward(c, h, seq[0])
-            for i in range(2, PACK):
-                exp(c, h, seq[i])
-                if seq[i - 1] in own:
-                    forward(c, h, seq[i - 1])
-            forward(c, h, seq[PACK - 1])
-            for a in helped:
-                assist_out(c, h, a)
+            first = c == 0 and h == 0
+            exp(c, h, 0)
+            exp(c, h, 1)
+            if first:
+                second_half()
+                m1(0, 0, 3)
+            forward(c, h, 0)
+            exp(c, h, 2)
+            forward(c, h, 1)
+            if h == 1 and c + 2 < CHUNKS:
+                turn(c + 2, 0)
+                turn(c + 2, 1)
+            if h == 1 or c > 0:
+                exp_halo(c, h)
+            if assisted(c, h):
+                assist(c, h, 0)
+            exp(c, h, 3)
+            forward(c, h, 2)
+            if h == 0 and c == 0:
+                exp_halo(c, h)
+            forward(c, h, 3)
+            if assisted(c, h):
+                pending.append(lambda: assist_out(c, h, 0))
 
         for c in range(CHUNKS):
-            if c == 0:
-                m1(c, 0, order[0][0])
-                m1(c, 0, order[0][1])
-            m1_halo(c, 0)
-            m1(c, 0, order[0][2])
-            m1(c, 0, order[0][3])
+            e = c - 1
+            if c > 0:
+                m1(c, 0, 2)
+                m1(c, 0, 3)
+                m1_halo(c, 0)
             front(c, 0)
             if c == 0:
-                left_pe(0)
-                left_pe(1)
-            grouped = []
-            if c + 2 < CHUNKS:
-                grouped = [turn_half(c + 2, 0, "s"), turn_half(c + 2, 1, "s")]
-            m1(c, 1, order[1][0])
-            m1(c, 1, order[1][1])
+                left_start()
+            m1(c, 1, 0)
+            m1(c, 1, 1)
             m1_halo(c, 1)
-            flux(c, 0, free[0][0])
+            flux(c, 0, 0)
+            flux(c, 0, 1)
             if c > 0:
-                quant_d(c - 1, 1)
+                quant_d(e, 1)
                 for t in range(3):
-                    m2(c - 1, t)
-            for a in free[0][1:]:
-                flux(c, 0, a)
-            m1(c, 1, order[1][2])
+                    m2(e, t)
+            m1(c, 1, 2)
+            flux(c, 0, 2)
+            flux(c, 0, 3)
+            for a in range(PACK):
+                flux_wrap(c, 0, a)
             left_flux(c, 0)
             if c > 0:
-                update(c - 1, 0)
-                m2(c - 1, 3)
-            diff_rest(c, 0)
-            m1(c, 1, order[1][3])
-            diff_first(c, 0)
-            if c > 0:
-                for t in range(1, PACK):
-                    update(c - 1, t)
-            scaled_u(c, 0)
-            scaled_u(c, 1)
+                for t in range(PACK):
+                    update(e, t)
+                    if t == 0:
+                        m2(e, 3)
+                    if t < POOL_U:
+                        scaled_u(c, t)
+            m1(c, 1, 3)
+            while pending:
+                pending.pop(0)()
+            diff(c, 0, 1, 2)
+            diff(c, 0, 0)
+            diff(c, 0, 3)
             front(c, 1)
-            if c + 1 < CHUNKS:
-                m1(c + 1, 0, order[0][0])
-                m1(c + 1, 0, order[0][1])
-            scaled_u(c, 2)
-            scaled_u(c, 3)
+            for t in range(POOL_U, PACK):
+                scaled_u(c, t)
+            while pending:
+                pending.pop(0)()
             if c > 0:
-                round_half(c - 1, 0)
-                round_half(c - 1, 1)
-            flux(c, 1, free[1][0])
-            quant_d(c, 0)
-            for half, g in enumerate(grouped):
-                quant_half(c + 2, half, g)
-            for a in free[1][1:]:
-                flux(c, 1, a)
+                round_half(e, 0)
+                round_half(e, 1)
+            if c + 1 < CHUNKS:
+                m1(c + 1, 0, 0)
+                m1(c + 1, 0, 1)
+            flux(c, 1, 0)
+            flux(c, 1, 1)
+            if c + 2 < CHUNKS:
+                quant_alpha(c + 2)
+            flux(c, 1, 2)
+            flux(c, 1, 3)
+            for a in range(PACK):
+                flux_wrap(c, 1, a)
             left_flux(c, 1)
-            if c > 1:
-                planes_half(c - 2, 0)
-                planes_half(c - 2, 1)
-            diff_rest(c, 1)
-            diff_first(c, 1)
+            quant_d(c, 0)
+            if c < CHUNKS - 1:
+                diff(c, 1, 1, 2)
+                diff(c, 1, 0)
+                if c > 0:
+                    planes(e)
+                diff(c, 1, 3)
 
         c = CHUNKS - 1
-        planes_half(c - 1, 0)
-        quant_d(c, 1)
-        planes_half(c - 1, 1)
+        diff(c, 1, 0)
+        diff(c, 1, 1, 2)
+        quant_d(c, 1, 0, 2)
+        m2(c, 0)
+        m2(c, 1)
+        diff(c, 1, 3)
+        planes(c - 1)
+        quant_d(c, 1, 2, 2)
+        m2(c, 2)
         for t in range(PACK):
-            m2(c, t)
             update(c, t)
+            if t == 0:
+                m2(c, 3)
         round_half(c, 0)
         round_half(c, 1)
-        planes_half(c, 0)
-        planes_half(c, 1)
+        planes(c, 0, 1)
+        planes(c, 1, 1)

@@ -22,14 +22,12 @@ PACK = 4
 CELLS = P * PACK
 CHUNKS = X // CELLS
 PASSES = Q // (P * PACK)
-PITCH = 136
+F_PITCH = 132
+X_PITCH = 136
 LEAD = 8
 HALF = N // 2
-POOL_U = 3
-
-
-def assisted(c, h):
-    return h == 1
+POOL_U = 2
+TURNS = {(0, 1): 2, (1, 0): 3}
 
 
 def tile_entropyclosuremomentkineticupwindstep_x2_kernel(
@@ -43,8 +41,8 @@ def tile_entropyclosuremomentkineticupwindstep_x2_kernel(
         single = ctx.enter_context(tc.tile_pool(name="single", bufs=1))
         work3 = ctx.enter_context(tc.tile_pool(name="work3", bufs=3))
         work4 = ctx.enter_context(tc.tile_pool(name="work4", bufs=4))
-        psum_eta = ctx.enter_context(tc.psum_pool(name="psum_eta", bufs=2))
-        psum_misc = ctx.enter_context(tc.psum_pool(name="psum_misc", bufs=3))
+        psum_eta = ctx.enter_context(tc.psum_pool(name="psum_eta", bufs=3))
+        psum_misc = ctx.enter_context(tc.psum_pool(name="psum_misc", bufs=2))
         psum_div = ctx.enter_context(tc.psum_pool(name="psum_div", bufs=3))
         ctx.enter_context(tc.manual_schedule())
 
@@ -174,99 +172,78 @@ def tile_entropyclosuremomentkineticupwindstep_x2_kernel(
                 stage1(h, a, codes[:, nxt, 0:P], scales[:, nxt, 0:P], halo[:, a, :])
             halo_t[c, h] = halo
 
+        F0 = 3 * F_PITCH - 1
+
+        def slots(tile, a, count, first, pitch, lead):
+            span = tile[:, a, first * pitch + lead : (first + count - 1) * pitch + lead + P]
+            if count == 1:
+                return span
+            whole = tile[:, a, lead : lead + (tile.shape[2] - lead) // pitch * pitch]
+            return whole.rearrange("p (t m) -> p t m", m=pitch)[:, first : first + count, 0:P]
+
         def exp(c, h, a):
             if a == 0:
-                f = work3.tile([P, PACK, PACK, PITCH], F32, name="f")
+                f = work3.tile([P, PACK, PACK * F_PITCH], F32, name="f")
                 f_t[c, h] = f
+            nc.scalar.activation(out=f_t[c, h][:, a, F0 : F0 + P], in_=eta_t[c, h, a][:, 0:P], func=ACT.Exp)
             nc.scalar.activation(
-                out=f_t[c, h][:, a, :, 0:P],
-                in_=eta_t[c, h, a][:].rearrange("p (t m) -> p t m", t=PACK),
+                out=slots(f_t[c, h], a, 3, 0, F_PITCH, 0), in_=eta_t[c, h, a][:, P:CELLS].rearrange("p (t m) -> p t m", t=3),
                 func=ACT.Exp,
             )
 
         def exp_halo(c, h):
-            nc.scalar.activation(out=f_t[c, h][:, :, 0, P : P + 1], in_=halo_t[c, h][:, :, 0:1], func=ACT.Exp)
+            nc.scalar.activation(out=f_t[c, h][:, :, F0 + P : F0 + P + 1], in_=halo_t[c, h][:, :, 0:1], func=ACT.Exp)
 
         def forward(c, h, a):
-            if a == 0 and assisted(c, h):
-                return
-            if (c, h) not in a_t:
+            if a == 0:
                 fw = work3.tile([P, PACK, PACK, P], F32, name="fw")
                 a_t[c, h] = fw
             j = h * PACK + a
             nc.scalar.activation(
-                out=a_t[c, h][:, a], in_=f_t[c, h][:, a, :, 0:P], func=ACT.Copy, scale=wpos[:, j : j + 1]
+                out=a_t[c, h][:, a, 0], in_=f_t[c, h][:, a, F0 : F0 + P], func=ACT.Copy, scale=wpos[:, j : j + 1]
             )
-
-        S3, S0 = LEAD, LEAD + P
-
-        def flux_wrap(c, h, a):
-            if a == 0 and assisted(c, h):
-                return
-            j = h * PACK + a
-            nc.vector.scalar_tensor_tensor(
-                out=x_t[c, h][:, a, S3 : S3 + P], in0=f_t[c, h][:, a, 0, 1 : P + 1], scalar=wneg[:, j : j + 1],
-                in1=a_t[c, h][:, a, 3, :], op0=ALU.mult, op1=ALU.add,
+            nc.scalar.activation(
+                out=a_t[c, h][:, a, 1:4], in_=slots(f_t[c, h], a, 3, 0, F_PITCH, 0), func=ACT.Copy,
+                scale=wpos[:, j : j + 1],
             )
-
-        def x_new(c, h):
-            if (c, h) not in x_t:
-                x = work4.tile([P, PACK, LEAD + CELLS], F32, name="x")
-                x_t[c, h] = x
 
         def flux(c, h, a):
-            if a == 0 and assisted(c, h):
-                return
-            x_new(c, h)
+            if a == 0:
+                x = work4.tile([P, PACK, LEAD + PACK * X_PITCH], F32, name="x")
+                x_t[c, h] = x
             j = h * PACK + a
-            f, fw, x = f_t[c, h], a_t[c, h], x_t[c, h]
             nc.vector.scalar_tensor_tensor(
-                out=x[:, a, S0 : S0 + 3 * P].rearrange("p (t m) -> p t m", t=3), in0=f[:, a, 1:4, 0:P],
-                scalar=wneg[:, j : j + 1], in1=fw[:, a, 0:3, :], op0=ALU.mult, op1=ALU.add,
+                out=slots(x_t[c, h], a, PACK, 0, X_PITCH, LEAD), in0=slots(f_t[c, h], a, PACK, 0, F_PITCH, 0),
+                scalar=wneg[:, j : j + 1], in1=a_t[c, h][:, a], op0=ALU.mult, op1=ALU.add,
             )
 
-        fl_t = {}
-
-        def assist(c, h, a):
-            f = f_t[c, h]
-            bank = psum_misc.tile([P, PACK, P], F32, name="fl", tag="misc")
-            pos, neg = diag[h]
-            nc.tensor.matmul(bank[:, 1:4, :], pos[:], f[:, a, 0:3, 0:P], start=True, stop=False)
-            nc.tensor.matmul(bank[:, 1:4, :], neg[:], f[:, a, 1:4, 0:P], start=False, stop=True)
-            nc.tensor.matmul(bank[:, 0, :], neg[:], f[:, a, 0, 1 : P + 1], start=True, stop=False)
-            nc.tensor.matmul(bank[:, 0, :], pos[:], f[:, a, 3, 0:P], start=False, stop=True)
-            fl_t[c, h] = bank
-
-        def assist_out(c, h, a):
-            x_new(c, h)
-            nc.scalar.copy(out=x_t[c, h][:, a, LEAD : LEAD + CELLS], in_=fl_t[c, h][:].rearrange("p t m -> p (t m)"))
+        X3 = LEAD + 3 * X_PITCH
 
         def left_flux(c, h):
-            dst = x_t[c, h][:, :, LEAD - 1 : LEAD]
+            dst = x_t[c, h][:, :, X3 - 1 : X3]
             if c > 0:
-                nc.gpsimd.tensor_copy(out=dst, in_=x_t[c - 1, h][:, :, S3 + P - 1 : S3 + P])
+                nc.gpsimd.tensor_copy(out=dst, in_=x_t[c - 1, h][:, :, X3 + P - 1 : X3 + P])
                 return
             cols = slice(h * PACK, (h + 1) * PACK)
             nc.gpsimd.tensor_tensor(out=l_pos[:, h], in0=f_last[:, h], in1=wpos[:, cols], op=ALU.mult)
             nc.gpsimd.tensor_tensor(
-                out=l_neg[:, h].unsqueeze(2), in0=f_t[0, h][:, :, 0, 0:1], in1=wneg[:, cols].unsqueeze(2), op=ALU.mult
+                out=l_neg[:, h].unsqueeze(2), in0=f_t[0, h][:, :, F0 : F0 + 1], in1=wneg[:, cols].unsqueeze(2), op=ALU.mult
             )
             nc.gpsimd.tensor_tensor(out=dst, in0=l_pos[:, h].unsqueeze(2), in1=l_neg[:, h].unsqueeze(2), op=ALU.add)
 
-        def diff(c, h, t, count=1):
+        def diff(c, h, t):
             if (c, h) not in d_t:
                 d = work3.tile([P, CELLS, PACK], BF16, name="d", align_bytes=64)
                 d_t[c, h] = d
             x = x_t[c, h]
-            here = S0 + t * P if t < 3 else S3
-            back = {0: S3 - 1, 1: S0, 3: S0 + 2 * P}[t]
-            width = count * P
-            runs = "p a (g i) -> p g a i"
+            here = LEAD + t * X_PITCH
+            back = here - X_PITCH if t > 0 else X3 - 1
             run = 8 if t == 0 else 4
+            runs = "p a (g i) -> p g a i"
             nc.vector.tensor_tensor(
-                out=d_t[c, h][:, t * P : t * P + width].rearrange("p (g i) a -> p g a i", i=run),
-                in0=x[:, :, here : here + width].rearrange(runs, i=run),
-                in1=x[:, :, back : back + width].rearrange(runs, i=run),
+                out=d_t[c, h][:, t * P : (t + 1) * P].rearrange("p (g i) a -> p g a i", i=run),
+                in0=x[:, :, here : here + P].rearrange(runs, i=run),
+                in1=x[:, :, back : back + P].rearrange(runs, i=run),
                 op=ALU.subtract,
             )
 
@@ -298,7 +275,12 @@ def tile_entropyclosuremomentkineticupwindstep_x2_kernel(
 
         def scaled_u(c, t):
             j = c * PACK + t
-            if t < POOL_U:
+            if c == 0:
+                up = single.tile([P, N], F32, name="up", tag="%s%d" % ("up" if t < POOL_U else "upa", t))
+                nc.vector.tensor_scalar(
+                    out=up[:], in0=ut[c][:, t], scalar1=rden[:, j : j + 1], scalar2=None, op0=ALU.mult
+                )
+            elif t < POOL_U:
                 up = single.tile([P, N], F32, name="up", tag="up%d" % t)
                 nc.gpsimd.tensor_scalar(
                     out=up[:], in0=ut[c][:, t], scalar1=rden[:, j : j + 1], scalar2=0.0, op0=ALU.mult, op1=ALU.add
@@ -384,21 +366,6 @@ def tile_entropyclosuremomentkineticupwindstep_x2_kernel(
                 for a in range(PACK):
                     stage1(h, a, lcodes[:], lscales[:], left[:, a, :])
                 nc.scalar.activation(out=f_last[:, h].unsqueeze(2), in_=left[:, :, P - 1 : P], func=ACT.Exp)
-            for t in range(POOL_U):
-                scaled_u(0, t)
-
-        pending = []
-        diag = {}
-        for h in range(PASSES):
-            pair = []
-            for sign, col in (("pos", wpos), ("neg", wneg)):
-                dg = keep.tile([P, P], F32, name="dg", tag="dg_%s_%d" % (sign, h))
-                nc.gpsimd.tensor_scalar(
-                    out=dg[:], in0=ident[:], scalar1=col[:, h * PACK : h * PACK + 1], scalar2=0.0,
-                    op0=ALU.mult, op1=ALU.add,
-                )
-                pair.append(dg)
-            diag[h] = pair
 
         def front(c, h):
             first = c == 0 and h == 0
@@ -407,30 +374,26 @@ def tile_entropyclosuremomentkineticupwindstep_x2_kernel(
             if first:
                 second_half()
                 m1(0, 0, 3)
+            if not first:
+                exp_halo(c, h)
             forward(c, h, 0)
             exp(c, h, 2)
-            forward(c, h, 1)
-            if h == 1 and c + 2 < CHUNKS:
-                turn(c + 2, 0)
-                turn(c + 2, 1)
-            if h == 1 or c > 0:
+            if first:
                 exp_halo(c, h)
-            if assisted(c, h):
-                assist(c, h, 0)
+            forward(c, h, 1)
+            if (c, h) in TURNS:
+                turn(TURNS[c, h], 0)
+                turn(TURNS[c, h], 1)
             exp(c, h, 3)
             forward(c, h, 2)
-            if h == 0 and c == 0:
-                exp_halo(c, h)
             forward(c, h, 3)
-            if assisted(c, h):
-                pending.append(lambda: assist_out(c, h, 0))
 
         for c in range(CHUNKS):
             e = c - 1
             if c > 0:
+                m1_halo(c, 0)
                 m1(c, 0, 2)
                 m1(c, 0, 3)
-                m1_halo(c, 0)
             front(c, 0)
             if c == 0:
                 left_start()
@@ -445,9 +408,9 @@ def tile_entropyclosuremomentkineticupwindstep_x2_kernel(
                     m2(e, t)
             m1(c, 1, 2)
             flux(c, 0, 2)
+            if c == 1:
+                quant_alpha(3)
             flux(c, 0, 3)
-            for a in range(PACK):
-                flux_wrap(c, 0, a)
             left_flux(c, 0)
             if c > 0:
                 for t in range(PACK):
@@ -457,17 +420,12 @@ def tile_entropyclosuremomentkineticupwindstep_x2_kernel(
                     if t < POOL_U:
                         scaled_u(c, t)
             m1(c, 1, 3)
-            while pending:
-                pending.pop(0)()
-            diff(c, 0, 1, 2)
-            diff(c, 0, 0)
-            diff(c, 0, 3)
+            for t in (1, 2, 3, 0):
+                diff(c, 0, t)
             front(c, 1)
-            for t in range(POOL_U, PACK):
-                scaled_u(c, t)
-            while pending:
-                pending.pop(0)()
             if c > 0:
+                for t in range(POOL_U, PACK):
+                    scaled_u(c, t)
                 round_half(e, 0)
                 round_half(e, 1)
             if c + 1 < CHUNKS:
@@ -475,24 +433,29 @@ def tile_entropyclosuremomentkineticupwindstep_x2_kernel(
                 m1(c + 1, 0, 1)
             flux(c, 1, 0)
             flux(c, 1, 1)
-            if c + 2 < CHUNKS:
-                quant_alpha(c + 2)
+            if c == 0:
+                quant_alpha(2)
+                scaled_u(0, 0)
+                scaled_u(0, 1)
             flux(c, 1, 2)
+            if c == 0:
+                scaled_u(0, 2)
+                scaled_u(0, 3)
             flux(c, 1, 3)
-            for a in range(PACK):
-                flux_wrap(c, 1, a)
             left_flux(c, 1)
             quant_d(c, 0)
             if c < CHUNKS - 1:
-                diff(c, 1, 1, 2)
-                diff(c, 1, 0)
+                diff(c, 1, 1)
+                diff(c, 1, 2)
+                diff(c, 1, 3)
                 if c > 0:
                     planes(e)
-                diff(c, 1, 3)
+                diff(c, 1, 0)
 
         c = CHUNKS - 1
+        diff(c, 1, 1)
         diff(c, 1, 0)
-        diff(c, 1, 1, 2)
+        diff(c, 1, 2)
         quant_d(c, 1, 0, 2)
         m2(c, 0)
         m2(c, 1)

from contextlib import ExitStack

import concourse.mybir as mybir
from concourse.masks import make_identity

X, N, Q = 2048, 512, 1024
FLOPS = 2 * (2 * X * N * Q)

F32 = mybir.dt.float32
BF16 = mybir.dt.bfloat16
I32 = mybir.dt.int32
U32 = mybir.dt.uint32
U8 = mybir.dt.uint8
FP8X4 = mybir.dt.float8_e4m3fn_x4
FP4X4 = mybir.dt.float4_e2m1fn_x4

ALU = mybir.AluOpType
ACT = mybir.ActivationFunctionType

P = 128
PACK = 4
CELLS = P * PACK
CHUNKS = X // CELLS
PASSES = Q // (P * PACK)
F_PITCH = 132
X_PITCH = 136
LEAD = 8
HALF = N // 2
POOL_U = 2
TURNS = {(0, 1): 2, (1, 0): 3}


def tile_entropyclosuremomentkineticupwindstep_x2_kernel(
    tc, alpha, m_words, m_scales, w, p_words, p_scales, u, sigma, out_0, out_1, out_2
):
    nc = tc.nc
    with ExitStack() as ctx:
        keep = ctx.enter_context(tc.tile_pool(name="keep", bufs=1))
        load = ctx.enter_context(tc.tile_pool(name="load", bufs=CHUNKS))
        work = ctx.enter_context(tc.tile_pool(name="work", bufs=2))
        single = ctx.enter_context(tc.tile_pool(name="single", bufs=1))
        work3 = ctx.enter_context(tc.tile_pool(name="work3", bufs=3))
        work4 = ctx.enter_context(tc.tile_pool(name="work4", bufs=4))
        psum_eta = ctx.enter_context(tc.psum_pool(name="psum_eta", bufs=3))
        psum_misc = ctx.enter_context(tc.psum_pool(name="psum_misc", bufs=2))
        psum_div = ctx.enter_context(tc.psum_pool(name="psum_div", bufs=3))
        ctx.enter_context(tc.manual_schedule())

        ident = keep.tile([P, P], F32, name="ident")
        m_raw = keep.tile([P, 2 * Q], U8, name="m_raw", align_bytes=64)
        m_plane = keep.tile([P, Q], U8, name="m_plane", align_bytes=64)
        mw = keep.tile([P, PASSES, PACK, 2 * P], U8, name="mw", align_bytes=64)
        ms = keep.tile([P, PASSES, PACK, P], U8, name="ms", align_bytes=64)
        pw = keep.tile([P, PASSES, 2 * N], U8, name="pw", align_bytes=64)
        ps = keep.tile([P, PASSES, N], U8, name="ps", align_bytes=64)
        w_sb = keep.tile([P, PASSES, 16], BF16, name="w_sb")
        s_sb = keep.tile([P, CHUNKS, 16], BF16, name="s_sb")
        wpos = keep.tile([P, PASSES * PACK], F32, name="wpos")
        wneg = keep.tile([P, PASSES * PACK], F32, name="wneg")
        s1 = keep.tile([P, CHUNKS * PACK], F32, name="s1")
        rden = keep.tile([P, CHUNKS * PACK], F32, name="rden")
        rneg = keep.tile([P, CHUNKS * PACK], F32, name="rneg")
        codes = keep.tile([P, CHUNKS, CELLS], U32, name="codes", align_bytes=64)
        scales = keep.tile([P, CHUNKS, CELLS], U8, name="scales", align_bytes=64)
        lcodes = keep.tile([P, P], U32, name="lcodes", align_bytes=64)
        lscales = keep.tile([P, P], U8, name="lscales", align_bytes=64)
        f_last = keep.tile([P, PASSES, PACK], F32, name="f_last")
        l_pos = keep.tile([P, PASSES, PACK], F32, name="l_pos")
        l_neg = keep.tile([P, PASSES, PACK], F32, name="l_neg")

        alpha_rows = alpha.rearrange("(c m t) k -> c m t k", m=P, t=PACK)
        u_rows = u.rearrange("(c m t) n -> c m t n", m=P, t=PACK)
        out_rows = out_0.rearrange("(c m t) n -> c m t n", m=P, t=PACK)

        al = [load.tile([P, PACK, N], BF16, name="al") for _ in range(CHUNKS)]
        al_left = keep.tile([P, N], BF16, name="al_left")
        ut = [load.tile([P, PACK, N], BF16, name="ut") for _ in range(CHUNKS)]

        nc.vector.memset(m_plane[:].bitcast(I32), 0)
        nc.vector.memset(ps[:].rearrange("p g n -> p (g n)").bitcast(I32), 0)
        make_identity(nc, ident[:])

        nc.sync.dma_start(out=al[0][:, 0:2, :], in_=alpha_rows[0, :, 0:2, :])
        nc.scalar.dma_start(out=w_sb[:, :, 0:PACK], in_=w.rearrange("(h p a) -> p h a", p=P, a=PACK))
        nc.sync.dma_start(out=al[0][:, 2:4, :], in_=alpha_rows[0, :, 2:4, :])
        nc.sync.dma_start(out=m_raw[:].bitcast(I32), in_=m_words[0].bitcast(I32))
        for quad in range(4):
            nc.scalar.dma_start(
                out=m_plane[32 * quad : 32 * quad + 4, :].bitcast(I32),
                in_=m_scales[0, 4 * quad : 4 * quad + 4, :].bitcast(I32),
            )
        nc.sync.dma_start(out=al_left[:], in_=alpha[X - P : X, :])
        nc.sync.dma_start(out=al[1][:], in_=alpha_rows[1])
        nc.scalar.dma_start(out=s_sb[:, :, 0:PACK], in_=sigma.rearrange("(c m t) -> m c t", m=P, t=PACK))
        nc.sync.dma_start(out=ut[0][:], in_=u_rows[0])
        nc.sync.dma_start(out=pw[:].bitcast(I32), in_=p_words.bitcast(I32).rearrange("g p b -> p g b"))
        for quad in range(4):
            nc.sync.dma_start(
                out=ps[32 * quad : 32 * quad + 4, :, :].bitcast(I32),
                in_=p_scales.bitcast(I32)[:, 4 * quad : 4 * quad + 4, :].rearrange("g r n -> r g n"),
            )
        for c in range(2, CHUNKS):
            nc.sync.dma_start(out=al[c][:], in_=alpha_rows[c])
            nc.sync.dma_start(out=ut[c - 1][:], in_=u_rows[c - 1])
        nc.sync.dma_start(out=ut[CHUNKS - 1][:], in_=u_rows[CHUNKS - 1])

        def permute_m(h, first, count):
            pick = slice(first, first + count)
            raw = m_raw[:, h * N * 2 : (h + 1) * N * 2].rearrange("p (m a b) -> p a m b", a=PACK, b=2)
            nc.vector.tensor_copy(
                out=mw[:, h, pick].rearrange("p a (m b) -> p a m b", b=2), in_=raw[:, pick]
            )
            plane = m_plane[:, h * N : (h + 1) * N].rearrange("p (m a) -> p a m", a=PACK)
            nc.vector.tensor_copy(out=ms[:, h, pick], in_=plane[:, pick])

        grouped_t = {}

        def turn(c, half):
            words = al[c][:].bitcast(F32)
            bank = psum_misc.tile([P, 2, 2, P], F32, name="bank", tag="misc")
            for t in range(2):
                for e in range(2):
                    nc.tensor.transpose(bank[:, t, e, :], words[:, 2 * half + t, e : N // 2 : 2], ident[:])
            if half == 0:
                grouped = work.tile([P, 2, 2 * P, PACK], BF16, name="grouped", align_bytes=64)
                grouped_t[c] = grouped
            nc.scalar.copy(
                out=grouped_t[c][:, half].bitcast(F32).rearrange("p (t m) e -> p t m e", t=2),
                in_=bank[:].rearrange("p t e m -> p t m e"),
            )

        def quant_alpha(c, first=0, count=2):
            cols = slice(first * 2 * P, (first + count) * 2 * P)
            nc.vector.quantize_mx(
                out=codes[:, c, cols].bitcast(FP8X4),
                scales=scales[:, c, cols],
                in_=grouped_t[c][:, first : first + count].rearrange("p s c t -> p (s c t)"),
            )

        lgrouped = keep.tile([P, P, PACK], BF16, name="lgrouped", align_bytes=64)

        def turn_left():
            words = al_left[:].bitcast(F32)
            bank = psum_misc.tile([P, 2, 2, P], F32, name="bank", tag="misc")
            for e in range(2):
                nc.tensor.transpose(bank[:, 0, e, :], words[:, e : N // 2 : 2], ident[:])
            nc.scalar.copy(out=lgrouped[:].bitcast(F32), in_=bank[:, 0].rearrange("p e m -> p m e"))

        def stage1(h, a, rhs, rhs_scale, bank):
            nc.tensor.matmul_mx(
                out=bank,
                lhsT=mw[:, h, a, :].bitcast(FP4X4),
                lhsT_scale=ms[:, h, a, :],
                rhs=rhs.bitcast(FP8X4),
                rhs_scale=rhs_scale,
                start=True,
                stop=True,
            )

        f_t, a_t, x_t, d_t, dc_t, ds_t = {}, {}, {}, {}, {}, {}
        eta_t, halo_t, up_t, r_t, rb_t, div_t, pl_t = {}, {}, {}, {}, {}, {}, {}

        def m1(c, h, a):
            eta = psum_eta.tile([P, CELLS], F32, name="eta")
            stage1(h, a, codes[:, c, :], scales[:, c, :], eta[:])
            eta_t[c, h, a] = eta

        def m1_halo(c, h):
            nxt = (c + 1) % CHUNKS
            halo = psum_misc.tile([P, PACK, P], F32, name="halo", tag="misc")
            for a in range(PACK):
                stage1(h, a, codes[:, nxt, 0:P], scales[:, nxt, 0:P], halo[:, a, :])
            halo_t[c, h] = halo

        F0 = 3 * F_PITCH - 1

        def slots(tile, a, count, first, pitch, lead):
            span = tile[:, a, first * pitch + lead : (first + count - 1) * pitch + lead + P]
            if count == 1:
                return span
            whole = tile[:, a, lead : lead + (tile.shape[2] - lead) // pitch * pitch]
            return whole.rearrange("p (t m) -> p t m", m=pitch)[:, first : first + count, 0:P]

        def exp(c, h, a):
            if a == 0:
                f = work3.tile([P, PACK, PACK * F_PITCH], F32, name="f")
                f_t[c, h] = f
            nc.scalar.activation(out=f_t[c, h][:, a, F0 : F0 + P], in_=eta_t[c, h, a][:, 0:P], func=ACT.Exp)
            nc.scalar.activation(
                out=slots(f_t[c, h], a, 3, 0, F_PITCH, 0), in_=eta_t[c, h, a][:, P:CELLS].rearrange("p (t m) -> p t m", t=3),
                func=ACT.Exp,
            )

        def exp_halo(c, h):
            nc.scalar.activation(out=f_t[c, h][:, :, F0 + P : F0 + P + 1], in_=halo_t[c, h][:, :, 0:1], func=ACT.Exp)

        def forward(c, h, a):
            if a == 0:
                fw = work3.tile([P, PACK, PACK, P], F32, name="fw")
                a_t[c, h] = fw
            j = h * PACK + a
            nc.scalar.activation(
                out=a_t[c, h][:, a, 0], in_=f_t[c, h][:, a, F0 : F0 + P], func=ACT.Copy, scale=wpos[:, j : j + 1]
            )
            nc.scalar.activation(
                out=a_t[c, h][:, a, 1:4], in_=slots(f_t[c, h], a, 3, 0, F_PITCH, 0), func=ACT.Copy,
                scale=wpos[:, j : j + 1],
            )

        def flux(c, h, a):
            if a == 0:
                x = work4.tile([P, PACK, LEAD + PACK * X_PITCH], F32, name="x")
                x_t[c, h] = x
            j = h * PACK + a
            nc.vector.scalar_tensor_tensor(
                out=slots(x_t[c, h], a, PACK, 0, X_PITCH, LEAD), in0=slots(f_t[c, h], a, PACK, 0, F_PITCH, 0),
                scalar=wneg[:, j : j + 1], in1=a_t[c, h][:, a], op0=ALU.mult, op1=ALU.add,
            )

        X3 = LEAD + 3 * X_PITCH

        def left_flux(c, h):
            dst = x_t[c, h][:, :, X3 - 1 : X3]
            if c > 0:
                nc.gpsimd.tensor_copy(out=dst, in_=x_t[c - 1, h][:, :, X3 + P - 1 : X3 + P])
                return
            cols = slice(h * PACK, (h + 1) * PACK)
            nc.gpsimd.tensor_tensor(out=l_pos[:, h], in0=f_last[:, h], in1=wpos[:, cols], op=ALU.mult)
            nc.gpsimd.tensor_tensor(
                out=l_neg[:, h].unsqueeze(2), in0=f_t[0, h][:, :, F0 : F0 + 1], in1=wneg[:, cols].unsqueeze(2), op=ALU.mult
            )
            nc.gpsimd.tensor_tensor(out=dst, in0=l_pos[:, h].unsqueeze(2), in1=l_neg[:, h].unsqueeze(2), op=ALU.add)

        def diff(c, h, t):
            if (c, h) not in d_t:
                d = work3.tile([P, CELLS, PACK], BF16, name="d", align_bytes=64)
                d_t[c, h] = d
            x = x_t[c, h]
            here = LEAD + t * X_PITCH
            back = here - X_PITCH if t > 0 else X3 - 1
            run = 8 if t == 0 else 4
            runs = "p a (g i) -> p g a i"
            nc.vector.tensor_tensor(
                out=d_t[c, h][:, t * P : (t + 1) * P].rearrange("p (g i) a -> p g a i", i=run),
                in0=x[:, :, here : here + P].rearrange(runs, i=run),
                in1=x[:, :, back : back + P].rearrange(runs, i=run),
                op=ALU.subtract,
            )

        def quant_d(c, h, first=0, count=PACK):
            if first == 0:
                dc = work4.tile([P, CELLS], U32, name="dc", align_bytes=64)
                ds = work4.tile([P, CELLS], U8, name="ds", align_bytes=64)
                dc_t[c, h], ds_t[c, h] = dc, ds
            cols = slice(first * P, (first + count) * P)
            nc.vector.quantize_mx(
                out=dc_t[c, h][:, cols].bitcast(FP8X4), scales=ds_t[c, h][:, cols],
                in_=d_t[c, h][:, cols].rearrange("p x a -> p (x a)"),
            )

        def m2(c, t):
            div = psum_div.tile([P, N], F32, name="div")
            cols = slice(t * P, (t + 1) * P)
            for h in range(PASSES):
                nc.tensor.matmul_mx(
                    out=div[:],
                    lhsT=dc_t[c, h][:, cols].bitcast(FP8X4),
                    lhsT_scale=ds_t[c, h][:, cols],
                    rhs=pw[:, h, :].bitcast(FP4X4),
                    rhs_scale=ps[:, h, :],
                    start=(h == 0),
                    stop=(h == PASSES - 1),
                )
            div_t[c, t] = div

        def scaled_u(c, t):
            j = c * PACK + t
            if c == 0:
                up = single.tile([P, N], F32, name="up", tag="%s%d" % ("up" if t < POOL_U else "upa", t))
                nc.vector.tensor_scalar(
                    out=up[:], in0=ut[c][:, t], scalar1=rden[:, j : j + 1], scalar2=None, op0=ALU.mult
                )
            elif t < POOL_U:
                up = single.tile([P, N], F32, name="up", tag="up%d" % t)
                nc.gpsimd.tensor_scalar(
                    out=up[:], in0=ut[c][:, t], scalar1=rden[:, j : j + 1], scalar2=0.0, op0=ALU.mult, op1=ALU.add
                )
            else:
                up = work.tile([P, N], F32, name="up", tag="up%d" % t)
                nc.scalar.activation(out=up[:], in_=ut[c][:, t], func=ACT.Copy, scale=rden[:, j : j + 1])
            up_t[c, t] = up

        def update(c, t):
            if t == 0:
                r = work.tile([P, PACK, N], F32, name="r")
                r_t[c] = r
            j = c * PACK + t
            nc.vector.scalar_tensor_tensor(
                out=r_t[c][:, t], in0=div_t[c, t][:], scalar=rneg[:, j : j + 1], in1=up_t[c, t][:],
                op0=ALU.mult, op1=ALU.add,
            )
            nc.sync.dma_start(out=out_rows[c, :, t, :], in_=r_t[c][:, t])

        def round_half(c, half):
            if half == 0:
                rb = work.tile([P, N, PACK], BF16, name="rb", align_bytes=64)
                rb_t[c] = rb
            cols = slice(half * HALF, (half + 1) * HALF)
            src = r_t[c][:, :, cols].rearrange("p t (g i) -> p g t i", i=4)
            dst = rb_t[c][:, cols].rearrange("p (g i) t -> p g t i", i=4)
            if half == 0 and c == CHUNKS - 1:
                nc.vector.tensor_copy(out=dst, in_=src)
            else:
                nc.scalar.copy(out=dst, in_=src)

        def planes(c, first=0, count=2):
            if first == 0:
                pc = work.tile([P, N], U32, name="pc", align_bytes=64)
                pq = work.tile([P, N], U8, name="pq", align_bytes=64)
                pl_t[c] = (pc, pq)
            pc, pq = pl_t[c]
            cols = slice(first * HALF, (first + count) * HALF)
            nc.vector.quantize_mx(
                out=pc[:, cols].bitcast(FP8X4), scales=pq[:, cols],
                in_=rb_t[c][:, cols].rearrange("p n t -> p (n t)"),
            )
            nc.sync.dma_start(
                out=out_1[c, :, cols, :].rearrange("p m t -> p (m t)").bitcast(I32), in_=pc[:, cols].bitcast(I32)
            )
            if first + count == 2:
                for quad in range(4):
                    nc.sync.dma_start(
                        out=out_2[c, 4 * quad : 4 * quad + 4, :].bitcast(I32),
                        in_=pq[32 * quad : 32 * quad + 4, :].bitcast(I32),
                    )

        w_view = w_sb[:, :, 0:PACK]
        nc.vector.tensor_scalar(out=wpos[:].rearrange("p (h a) -> p h a", a=PACK), in0=w_view, scalar1=0.0, scalar2=None, op0=ALU.max)
        nc.vector.tensor_scalar(out=wneg[:].rearrange("p (h a) -> p h a", a=PACK), in0=w_view, scalar1=0.0, scalar2=None, op0=ALU.min)
        s_view = s_sb[:, :, 0:PACK]
        turn(0, 0)
        turn(0, 1)
        permute_m(0, 0, 2)
        quant_alpha(0, 0, 1)
        quant_alpha(0, 1, 1)
        turn_left()
        for a in range(2):
            m1(0, 0, a)
        permute_m(0, 2, 2)
        nc.vector.quantize_mx(out=lcodes[:].bitcast(FP8X4), scales=lscales[:], in_=lgrouped[:].rearrange("p c t -> p (c t)"))
        nc.vector.tensor_scalar(out=s1[:].rearrange("p (c t) -> p c t", t=PACK), in0=s_view, scalar1=1.0, scalar2=None, op0=ALU.add)
        m1(0, 0, 2)

        def second_half():
            turn(1, 0)
            turn(1, 1)
            permute_m(1, 0, PACK)
            nc.vector.reciprocal(out=rden[:], in_=s1[:])
            quant_alpha(1)
            m1_halo(0, 0)
            nc.vector.tensor_scalar(out=rneg[:], in0=rden[:], scalar1=-0.5, scalar2=None, op0=ALU.mult)

        def left_start():
            for h in range(PASSES):
                left = psum_misc.tile([P, PACK, P], F32, name="halo", tag="misc")
                for a in range(PACK):
                    stage1(h, a, lcodes[:], lscales[:], left[:, a, :])
                nc.scalar.activation(out=f_last[:, h].unsqueeze(2), in_=left[:, :, P - 1 : P], func=ACT.Exp)

        def front(c, h):
            first = c == 0 and h == 0
            exp(c, h, 0)
            exp(c, h, 1)
            if first:
                second_half()
                m1(0, 0, 3)
            if not first:
                exp_halo(c, h)
            forward(c, h, 0)
            exp(c, h, 2)
            if first:
                exp_halo(c, h)
            forward(c, h, 1)
            if (c, h) in TURNS:
                turn(TURNS[c, h], 0)
                turn(TURNS[c, h], 1)
            exp(c, h, 3)
            forward(c, h, 2)
            forward(c, h, 3)

        for c in range(CHUNKS):
            e = c - 1
            if c > 0:
                m1_halo(c, 0)
                m1(c, 0, 2)
                m1(c, 0, 3)
            front(c, 0)
            if c == 0:
                left_start()
            m1(c, 1, 0)
            m1(c, 1, 1)
            m1_halo(c, 1)
            flux(c, 0, 0)
            flux(c, 0, 1)
            if c > 0:
                quant_d(e, 1)
                for t in range(3):
                    m2(e, t)
            m1(c, 1, 2)
            flux(c, 0, 2)
            if c == 1:
                quant_alpha(3)
            flux(c, 0, 3)
            left_flux(c, 0)
            if c > 0:
                for t in range(PACK):
                    update(e, t)
                    if t == 0:
                        m2(e, 3)
                    if t < POOL_U:
                        scaled_u(c, t)
            m1(c, 1, 3)
            for t in (1, 2, 3, 0):
                diff(c, 0, t)
            front(c, 1)
            if c > 0:
                for t in range(POOL_U, PACK):
                    scaled_u(c, t)
                round_half(e, 0)
                round_half(e, 1)
            if c + 1 < CHUNKS:
                m1(c + 1, 0, 0)
                m1(c + 1, 0, 1)
            flux(c, 1, 0)
            flux(c, 1, 1)
            if c == 0:
                quant_alpha(2)
                scaled_u(0, 0)
                scaled_u(0, 1)
            flux(c, 1, 2)
            if c == 0:
                scaled_u(0, 2)
                scaled_u(0, 3)
            flux(c, 1, 3)
            left_flux(c, 1)
            quant_d(c, 0)
            if c < CHUNKS - 1:
                diff(c, 1, 1)
                diff(c, 1, 2)
                diff(c, 1, 3)
                if c > 0:
                    planes(e)
                diff(c, 1, 0)

        c = CHUNKS - 1
        diff(c, 1, 1)
        diff(c, 1, 0)
        diff(c, 1, 2)
        quant_d(c, 1, 0, 2)
        m2(c, 0)
        m2(c, 1)
        diff(c, 1, 3)
        planes(c - 1)
        quant_d(c, 1, 2, 2)
        m2(c, 2)
        for t in range(PACK):
            update(c, t)
            if t == 0:
                m2(c, 3)
        round_half(c, 0)
        round_half(c, 1)
        planes(c, 0, 1)
        planes(c, 1, 1)
